import numpy as np
import ml_dtypes


def mxq(x, axis, fmt="e4m3"):
    dtype, down = {"e4m3": (ml_dtypes.float8_e4m3fn, 7), "e5m2": (ml_dtypes.float8_e5m2, 14)}[fmt]
    v = np.moveaxis(np.asarray(x, np.float32).astype(ml_dtypes.bfloat16).astype(np.float64), axis, -1)
    blocks = v.reshape(v.shape[:-1] + (-1, 32))
    amax = np.abs(blocks).max(-1, keepdims=True)
    byte = np.maximum(np.where(amax > 0, np.frexp(amax)[1] - 1 + 127, 0) - down, 1)
    scale = np.exp2(byte - 127.0)
    codes = (blocks / scale).astype(np.float32).astype(dtype).astype(np.float64)
    return np.moveaxis((codes * scale).reshape(v.shape), -1, axis)


WIDE = False


def mx_kscale(k):
    if not WIDE:
        return np.ones(k)
    levels = np.array([10, -10, 5, -5, 0])
    if k % 512:
        return np.exp2(np.random.permutation(np.resize(levels, k // 32))).repeat(32)
    a = np.empty((k // 512, 16))
    for p in range(k // 512):
        a[p, :8] = np.random.permutation(np.resize(levels, 8))
        for g in range(8):
            far = levels[np.abs(levels - a[p, g]) >= 10]
            a[p, g + 8] = far[np.random.randint(len(far))]
    return np.exp2(a.ravel()).repeat(32)


def f64(x):
    return np.asarray(x).astype(np.float64)


def striped(idx):
    return np.tile(idx.reshape(-1, 16).T, (8, 1)).astype(np.uint16)


def unstriped(offs):
    return offs[:16].T.reshape(-1).astype(np.int64)


def sigmoid(v):
    return 1.0 / (1.0 + np.exp(-np.maximum(v, -700.0)))


K, T, D, S, V, N = 512, 4096, 2, 1536, 768, 256


def setup_inputs():
    n = np.random.standard_normal
    s = mx_kscale(K)[:, None]
    return {
        "xT": (n((K, T)) * s).astype(np.float32),
        "w": (n((D, K, N)) / np.sqrt(K) / s[None]).astype(np.float32),
        "b": (0.3 * n((N, 1))).astype(np.float32),
        "offs": striped(np.random.permutation(T)[:S]),
    }


def reference(xT, w, b, offs):
    idx = unstriped(offs)
    xq = mxq(f64(xT)[:, idx], 0, "e4m3")
    wq = mxq(f64(w), 1, "e4m3")
    y0 = wq[0].T @ xq[:, :V]
    y1 = wq[1].T @ xq[:, V:]
    return y0 * sigmoid(y1 + f64(b))

@@ -1,0 +1,134 @@
+from contextlib import ExitStack
+
+import concourse.mybir as mybir
+
+K, T, S, V, N = 512, 4096, 1536, 768, 256
+FLOPS = 2 * K * N * S
+
+F32 = mybir.dt.float32
+BF16 = mybir.dt.bfloat16
+U16 = mybir.dt.uint16
+U32 = mybir.dt.uint32
+U8 = mybir.dt.uint8
+FP8X4 = mybir.dt.float8_e4m3fn_x4
+MULT, ADD = mybir.AluOpType.mult, mybir.AluOpType.add
+SIGMOID = mybir.ActivationFunctionType.Sigmoid
+
+P = 128
+J = 4
+C = 512
+M = 128
+
+
+def tile_picked_pair_lin_gate_sub_e_kernel(tc, xT, w, b, offs, out):
+    nc = tc.nc
+    x_rows = xT.rearrange("(p j) t -> p j t", j=J)
+
+    with ExitStack() as ctx:
+        keep = ctx.enter_context(tc.tile_pool(name="keep", bufs=1))
+        psum = ctx.enter_context(tc.psum_pool(name="psum", bufs=1))
+
+        list_sb = keep.tile([P, S // 16], U16, name="list_sb")
+        planes = [keep.tile([P, T], F32, name=f"plane{j}") for j in range(J)]
+        w_raw = [keep.tile([P, J, N], F32, name=f"w_raw{d}") for d in range(2)]
+        bias = [keep.tile([P, 1], F32, name=f"bias{m}") for m in range(2)]
+        nc.sync.dma_start(list_sb[:], offs)
+        for j in range(J):
+            nc.sync.dma_start(planes[j][:], x_rows[:, j, :])
+        for d in (1, 0):
+            nc.sync.dma_start(w_raw[d][:], w[d].rearrange("(p j) n -> p j n", j=J))
+        for m in range(2):
+            nc.sync.dma_start(bias[m][:], b[m * M : (m + 1) * M, :])
+
+        warm = keep.tile([P, 1], F32, name="warm")
+        warm_out = keep.tile([P, 1], F32, name="warm_out")
+        nc.vector.memset(warm[:], 0.0)
+        nc.scalar.activation(warm_out[:], warm[:], SIGMOID)
+
+        starts = {"z": 0, "y": C, "x": 2 * C}
+
+        def picks(s):
+            return list_sb[:, starts[s] // 16 : (starts[s] + C) // 16]
+
+        early = {s: keep.tile([P, 2, C], F32, name=f"early_{s}") for s in "zyx"}
+        late = {s: keep.tile([P, 2, C], F32, name=f"late_{s}") for s in "yx"}
+        grouped = {s: keep.tile([P, C, J], BF16, name=f"grouped_{s}", tag=f"turn_{s}", align_bytes=64) for s in "zyx"}
+        codes = {s: keep.tile([P, C], U32, name=f"codes_{s}", align_bytes=64) for s in "zyx"}
+        scales = {s: keep.tile([P, C], U8, name=f"scales_{s}", align_bytes=64) for s in "zyx"}
+
+        for j in range(2):
+            for s in "zyx":
+                nc.vector.tensor_copy(early[s][:, j, :], planes[j][:].indirect(picks(s)))
+        for s in "zyx":
+            nc.scalar.copy(grouped[s][:, :, 0:2], early[s][:].rearrange("p u n -> p n u"))
+        for j in range(2, J):
+            for s in "xy":
+                nc.vector.tensor_copy(late[s][:, j - 2, :], planes[j][:].indirect(picks(s)))
+            nc.vector.tensor_copy(grouped["z"][:, :, j], planes[j][:].indirect(picks("z")))
+
+        w_grouped = [keep.tile([P, N, J], BF16, name=f"w_grouped{d}", align_bytes=64) for d in range(2)]
+        w_codes = {}
+        w_scales = [keep.tile([P, N], U8, name=f"w_scales{d}", align_bytes=64) for d in range(2)]
+        for d in (1, 0):
+            nc.gpsimd.tensor_scalar(w_grouped[d][:], w_raw[d][:].rearrange("p j n -> p n j"), 1.0, 0.0, MULT, ADD)
+
+        def quantize(codes_t, scales_t, grouped_t, c0, c1):
+            nc.vector.quantize_mx(
+                out=codes_t[:, c0:c1].bitcast(FP8X4),
+                scales=scales_t[:, c0:c1],
+                in_=grouped_t[:].rearrange("p n j -> p (n j)")[:, J * c0 : J * c1],
+            )
+
+        def multiply(acc, d, m, s, c0, c1):
+            cols = slice(m * M, (m + 1) * M)
+            nc.tensor.matmul_mx(
+                out=acc,
+                lhsT=w_codes[d][:, cols].bitcast(FP8X4),
+                lhsT_scale=w_scales[d][:, cols],
+                rhs=codes[s][:, c0:c1].bitcast(FP8X4),
+                rhs_scale=scales[s][:, c0:c1],
+                start=True,
+                stop=True,
+            )
+
+        gate = [keep.tile([P, V], F32, name=f"gate{m}") for m in range(2)]
+        result = [keep.tile([P, V], F32, name=f"result{m}") for m in range(2)]
+        HALF = C // 2
+
+        for s in "xy":
+            nc.scalar.copy(grouped[s][:, :, 2:4], late[s][:].rearrange("p u n -> p n u"))
+
+        quantize(codes["x"], scales["x"], grouped["x"], 0, C)
+        w_codes[1] = keep.tile([P, N], U32, name="w_codes1", tag="turn_x", align_bytes=64)
+        quantize(w_codes[1], w_scales[1], w_grouped[1], 0, N)
+        for m in range(2):
+            acc = psum.tile([P, C], F32, name=f"y1x{m}")
+            multiply(acc[:], 1, m, "x", 0, C)
+            nc.scalar.activation(gate[m][:, HALF:V], acc[:], SIGMOID, bias=bias[m][:])
+        quantize(codes["y"], scales["y"], grouped["y"], 0, C)
+        w_codes[0] = keep.tile([P, N], U32, name="w_codes0", tag="turn_y", align_bytes=64)
+        quantize(w_codes[0], w_scales[0], w_grouped[0], 0, N)
+        y0y = [psum.tile([P, HALF], F32, name=f"y0y{m}") for m in range(2)]
+        for m in range(2):
+            multiply(y0y[m][:], 0, m, "y", 0, HALF)
+        for m in range(2):
+            acc = psum.tile([P, HALF], F32, name=f"y1y{m}")
+            multiply(acc[:], 1, m, "y", HALF, C)
+            nc.scalar.activation(gate[m][:, 0:HALF], acc[:], SIGMOID, bias=bias[m][:])
+        y0z = [psum.tile([P, C], F32, name=f"y0z{m}") for m in range(2)]
+        for h in (1, 0):
+            c0, c1 = h * HALF, (h + 1) * HALF
+            quantize(codes["z"], scales["z"], grouped["z"], c0, c1)
+            for m in range(2):
+                multiply(y0z[m][:, c0:c1], 0, m, "z", c0, c1)
+
+        def finish(acc, m, c0):
+            cols = slice(c0, c0 + HALF)
+            nc.vector.tensor_tensor(result[m][:, cols], acc, gate[m][:, cols], MULT)
+            nc.sync.dma_start(out[m * M : (m + 1) * M, cols], result[m][:, cols])
+
+        for m in range(2):
+            finish(y0y[m][:], m, C)
+        for h in (1, 0):
+            for m in range(2):
+                finish(y0z[m][:, h * HALF : (h + 1) * HALF], m, h * HALF)

@@ -11,13 +11,16 @@ U16 = mybir.dt.uint16
 U32 = mybir.dt.uint32
 U8 = mybir.dt.uint8
 FP8X4 = mybir.dt.float8_e4m3fn_x4
-MULT, ADD = mybir.AluOpType.mult, mybir.AluOpType.add
+MULT = mybir.AluOpType.mult
 SIGMOID = mybir.ActivationFunctionType.Sigmoid
+COPY = mybir.ActivationFunctionType.Copy
 
 P = 128
 J = 4
 C = 512
 M = 128
+HALF = C // 2
+CHUNKS = [[2048,2048],[2048,2048],[2048,1024,1024],[2048,1024,512,512]]
 
 
 def tile_picked_pair_lin_gate_sub_e_kernel(tc, xT, w, b, offs, out):
@@ -30,11 +33,19 @@ def tile_picked_pair_lin_gate_sub_e_kernel(tc, xT, w, b, offs, out):
 
         list_sb = keep.tile([P, S // 16], U16, name="list_sb")
         planes = [keep.tile([P, T], F32, name=f"plane{j}") for j in range(J)]
+        rounded = [keep.tile([P, T], BF16, name=f"rounded{j}") for j in range(J)]
         w_raw = [keep.tile([P, J, N], F32, name=f"w_raw{d}") for d in range(2)]
         bias = [keep.tile([P, 1], F32, name=f"bias{m}") for m in range(2)]
-        nc.sync.dma_start(list_sb[:], offs)
+
+        def spans(j):
+            edges = [sum(CHUNKS[j][:i]) for i in range(len(CHUNKS[j]) + 1)]
+            return [slice(a, z) for a, z in zip(edges, edges[1:])]
+
         for j in range(J):
-            nc.sync.dma_start(planes[j][:], x_rows[:, j, :])
+            for i, cols in enumerate(spans(j)):
+                nc.sync.dma_start(planes[j][:, cols], x_rows[:, j, cols])
+                if (j, i) == (0, 0):
+                    nc.sync.dma_start(list_sb[:], offs)
         for d in (1, 0):
             nc.sync.dma_start(w_raw[d][:], w[d].rearrange("(p j) n -> p j n", j=J))
         for m in range(2):
@@ -50,27 +61,25 @@ def tile_picked_pair_lin_gate_sub_e_kernel(tc, xT, w, b, offs, out):
         def picks(s):
             return list_sb[:, starts[s] // 16 : (starts[s] + C) // 16]
 
-        early = {s: keep.tile([P, 2, C], F32, name=f"early_{s}") for s in "zyx"}
-        late = {s: keep.tile([P, 2, C], F32, name=f"late_{s}") for s in "yx"}
-        grouped = {s: keep.tile([P, C, J], BF16, name=f"grouped_{s}", tag=f"turn_{s}", align_bytes=64) for s in "zyx"}
+        grouped = {s: keep.tile([P, C, J], BF16, name=f"grouped_{s}", align_bytes=64) for s in "zyx"}
         codes = {s: keep.tile([P, C], U32, name=f"codes_{s}", align_bytes=64) for s in "zyx"}
         scales = {s: keep.tile([P, C], U8, name=f"scales_{s}", align_bytes=64) for s in "zyx"}
-
-        for j in range(2):
-            for s in "zyx":
-                nc.vector.tensor_copy(early[s][:, j, :], planes[j][:].indirect(picks(s)))
-        for s in "zyx":
-            nc.scalar.copy(grouped[s][:, :, 0:2], early[s][:].rearrange("p u n -> p n u"))
-        for j in range(2, J):
-            for s in "xy":
-                nc.vector.tensor_copy(late[s][:, j - 2, :], planes[j][:].indirect(picks(s)))
-            nc.vector.tensor_copy(grouped["z"][:, :, j], planes[j][:].indirect(picks("z")))
-
         w_grouped = [keep.tile([P, N, J], BF16, name=f"w_grouped{d}", align_bytes=64) for d in range(2)]
-        w_codes = {}
+        w_codes = [keep.tile([P, N], U32, name=f"w_codes{d}", align_bytes=64) for d in range(2)]
         w_scales = [keep.tile([P, N], U8, name=f"w_scales{d}", align_bytes=64) for d in range(2)]
-        for d in (1, 0):
-            nc.gpsimd.tensor_scalar(w_grouped[d][:], w_raw[d][:].rearrange("p j n -> p n j"), 1.0, 0.0, MULT, ADD)
+
+        for j in range(J):
+            for cols in spans(j):
+                nc.vector.tensor_copy(rounded[j][:, cols], planes[j][:, cols])
+            nc.vector.tensor_copy(grouped["y"][:, :, j], planes[j][:].indirect(picks("y")))
+            for s in "xz":
+                nc.scalar.activation(grouped[s][:, :, j], rounded[j][:].indirect(picks(s)), COPY)
+
+        def cast_w(d):
+            nc.vector.tensor_copy(
+                w_grouped[d][:].rearrange("p (c i) j -> p c j i", i=4),
+                w_raw[d][:].rearrange("p j (c i) -> p c j i", i=4),
+            )
 
         def quantize(codes_t, scales_t, grouped_t, c0, c1):
             nc.vector.quantize_mx(
@@ -93,42 +102,37 @@ def tile_picked_pair_lin_gate_sub_e_kernel(tc, xT, w, b, offs, out):
 
         gate = [keep.tile([P, V], F32, name=f"gate{m}") for m in range(2)]
         result = [keep.tile([P, V], F32, name=f"result{m}") for m in range(2)]
-        HALF = C // 2
 
-        for s in "xy":
-            nc.scalar.copy(grouped[s][:, :, 2:4], late[s][:].rearrange("p u n -> p n u"))
-
+        cast_w(1)
         quantize(codes["x"], scales["x"], grouped["x"], 0, C)
-        w_codes[1] = keep.tile([P, N], U32, name="w_codes1", tag="turn_x", align_bytes=64)
         quantize(w_codes[1], w_scales[1], w_grouped[1], 0, N)
+        y1x = [psum.tile([P, C], F32, name=f"y1x{m}") for m in range(2)]
         for m in range(2):
-            acc = psum.tile([P, C], F32, name=f"y1x{m}")
-            multiply(acc[:], 1, m, "x", 0, C)
-            nc.scalar.activation(gate[m][:, HALF:V], acc[:], SIGMOID, bias=bias[m][:])
+            multiply(y1x[m][:], 1, m, "x", 0, C)
+        cast_w(0)
         quantize(codes["y"], scales["y"], grouped["y"], 0, C)
-        w_codes[0] = keep.tile([P, N], U32, name="w_codes0", tag="turn_y", align_bytes=64)
         quantize(w_codes[0], w_scales[0], w_grouped[0], 0, N)
+        y1y = [psum.tile([P, HALF], F32, name=f"y1y{m}") for m in range(2)]
         y0y = [psum.tile([P, HALF], F32, name=f"y0y{m}") for m in range(2)]
+        for m in range(2):
+            multiply(y1y[m][:], 1, m, "y", HALF, C)
         for m in range(2):
             multiply(y0y[m][:], 0, m, "y", 0, HALF)
         for m in range(2):
-            acc = psum.tile([P, HALF], F32, name=f"y1y{m}")
-            multiply(acc[:], 1, m, "y", HALF, C)
-            nc.scalar.activation(gate[m][:, 0:HALF], acc[:], SIGMOID, bias=bias[m][:])
+            nc.scalar.activation(gate[m][:, HALF:V], y1x[m][:], SIGMOID, bias=bias[m][:])
+        for m in range(2):
+            nc.scalar.activation(gate[m][:, 0:HALF], y1y[m][:], SIGMOID, bias=bias[m][:])
         y0z = [psum.tile([P, C], F32, name=f"y0z{m}") for m in range(2)]
-        for h in (1, 0):
-            c0, c1 = h * HALF, (h + 1) * HALF
-            quantize(codes["z"], scales["z"], grouped["z"], c0, c1)
-            for m in range(2):
-                multiply(y0z[m][:, c0:c1], 0, m, "z", c0, c1)
+        quantize(codes["z"], scales["z"], grouped["z"], 0, C)
+        for m in range(2):
+            multiply(y0z[m][:], 0, m, "z", 0, C)
 
-        def finish(acc, m, c0):
-            cols = slice(c0, c0 + HALF)
+        def finish(acc, m, c0, c1):
+            cols = slice(c0, c1)
             nc.vector.tensor_tensor(result[m][:, cols], acc, gate[m][:, cols], MULT)
             nc.sync.dma_start(out[m * M : (m + 1) * M, cols], result[m][:, cols])
 
         for m in range(2):
-            finish(y0y[m][:], m, C)
-        for h in (1, 0):
-            for m in range(2):
-                finish(y0z[m][:, h * HALF : (h + 1) * HALF], m, h * HALF)
+            finish(y0y[m][:], m, C, V)
+        for m in range(2):
+            finish(y0z[m][:], m, 0, C)

@@ -20,6 +20,7 @@ J = 4
 C = 512
 M = 128
 HALF = C // 2
+ORDER = (0, 2, 3, 1)
 CHUNKS = [[2048,2048],[2048,2048],[2048,1024,1024],[2048,1024,512,512]]
 
 
@@ -34,17 +35,17 @@ def tile_picked_pair_lin_gate_sub_e_kernel(tc, xT, w, b, offs, out):
         list_sb = keep.tile([P, S // 16], U16, name="list_sb")
         planes = [keep.tile([P, T], F32, name=f"plane{j}") for j in range(J)]
         rounded = [keep.tile([P, T], BF16, name=f"rounded{j}") for j in range(J)]
-        w_raw = [keep.tile([P, J, N], F32, name=f"w_raw{d}") for d in range(2)]
+        w_raw = [keep.tile([P, J, N], F32, name=f"w_raw{d}", tag=f"side{d}", align_bytes=64) for d in range(2)]
         bias = [keep.tile([P, 1], F32, name=f"bias{m}") for m in range(2)]
 
         def spans(j):
             edges = [sum(CHUNKS[j][:i]) for i in range(len(CHUNKS[j]) + 1)]
             return [slice(a, z) for a, z in zip(edges, edges[1:])]
 
-        for j in range(J):
-            for i, cols in enumerate(spans(j)):
+        for step, j in enumerate(ORDER):
+            for i, cols in enumerate(spans(step)):
                 nc.sync.dma_start(planes[j][:, cols], x_rows[:, j, cols])
-                if (j, i) == (0, 0):
+                if (step, i) == (0, 0):
                     nc.sync.dma_start(list_sb[:], offs)
         for d in (1, 0):
             nc.sync.dma_start(w_raw[d][:], w[d].rearrange("(p j) n -> p j n", j=J))
@@ -56,76 +57,94 @@ def tile_picked_pair_lin_gate_sub_e_kernel(tc, xT, w, b, offs, out):
         nc.vector.memset(warm[:], 0.0)
         nc.scalar.activation(warm_out[:], warm[:], SIGMOID)
 
-        starts = {"z": 0, "y": C, "x": 2 * C}
+        def picks(a, z):
+            return list_sb[:, a // 16 : z // 16]
 
-        def picks(s):
-            return list_sb[:, starts[s] // 16 : (starts[s] + C) // 16]
-
-        grouped = {s: keep.tile([P, C, J], BF16, name=f"grouped_{s}", align_bytes=64) for s in "zyx"}
-        codes = {s: keep.tile([P, C], U32, name=f"codes_{s}", align_bytes=64) for s in "zyx"}
-        scales = {s: keep.tile([P, C], U8, name=f"scales_{s}", align_bytes=64) for s in "zyx"}
-        w_grouped = [keep.tile([P, N, J], BF16, name=f"w_grouped{d}", align_bytes=64) for d in range(2)]
+        grouped = keep.tile([P, S * J], BF16, name="grouped", align_bytes=64)
+        by_entry = grouped[:].rearrange("p (n j) -> p n j", j=J)
+        tail_plain = keep.tile([P, 2, HALF], BF16, name="tail_plain")
+        codes = {}
+        scales = [keep.tile([P, V], U8, name=f"scales{d}", align_bytes=64) for d in range(2)]
         w_codes = [keep.tile([P, N], U32, name=f"w_codes{d}", align_bytes=64) for d in range(2)]
         w_scales = [keep.tile([P, N], U8, name=f"w_scales{d}", align_bytes=64) for d in range(2)]
 
-        for j in range(J):
-            for cols in spans(j):
+        for step, j in enumerate(ORDER):
+            for cols in spans(step):
                 nc.vector.tensor_copy(rounded[j][:, cols], planes[j][:, cols])
-            nc.vector.tensor_copy(grouped["y"][:, :, j], planes[j][:].indirect(picks("y")))
-            for s in "xz":
-                nc.scalar.activation(grouped[s][:, :, j], rounded[j][:].indirect(picks(s)), COPY)
+            if j < 2:
+                nc.vector.tensor_copy(tail_plain[:, j, :], planes[j][:].indirect(picks(S - HALF, S)))
+                shares = ((640, 1280), (0, 640))
+            else:
+                nc.vector.tensor_copy(by_entry[:, S - C : S, j], planes[j][:].indirect(picks(S - C, S)))
+                shares = ((C, 2 * C), (0, C))
+            for a, z in shares:
+                nc.scalar.activation(by_entry[:, a:z, j], rounded[j][:].indirect(picks(a, z)), COPY)
+        nc.vector.tensor_copy(by_entry[:, S - HALF : S, 0:2], tail_plain[:].rearrange("p u n -> p n u"))
+
+        w_grouped = {}
 
         def cast_w(d):
+            w_grouped[d] = keep.tile([P, N, J], BF16, name=f"w_grouped{d}", tag="w_grouped", align_bytes=64)
             nc.vector.tensor_copy(
                 w_grouped[d][:].rearrange("p (c i) j -> p c j i", i=4),
                 w_raw[d][:].rearrange("p j (c i) -> p c j i", i=4),
             )
+            codes[d] = keep.tile([P, V], U32, name=f"codes{d}", tag=f"side{d}", align_bytes=64)
 
-        def quantize(codes_t, scales_t, grouped_t, c0, c1):
+        def quantize_w(d):
             nc.vector.quantize_mx(
-                out=codes_t[:, c0:c1].bitcast(FP8X4),
-                scales=scales_t[:, c0:c1],
-                in_=grouped_t[:].rearrange("p n j -> p (n j)")[:, J * c0 : J * c1],
+                out=w_codes[d][:].bitcast(FP8X4),
+                scales=w_scales[d][:],
+                in_=w_grouped[d][:].rearrange("p n j -> p (n j)"),
             )
 
-        def multiply(acc, d, m, s, c0, c1):
+        def quantize(d, a, z):
+            nc.vector.quantize_mx(
+                out=codes[d][:, a:z].bitcast(FP8X4),
+                scales=scales[d][:, a:z],
+                in_=grouped[:, J * (d * V + a) : J * (d * V + z)],
+            )
+
+        def multiply(acc, d, m, a, z):
             cols = slice(m * M, (m + 1) * M)
             nc.tensor.matmul_mx(
                 out=acc,
                 lhsT=w_codes[d][:, cols].bitcast(FP8X4),
                 lhsT_scale=w_scales[d][:, cols],
-                rhs=codes[s][:, c0:c1].bitcast(FP8X4),
-                rhs_scale=scales[s][:, c0:c1],
+                rhs=codes[d][:, a:z].bitcast(FP8X4),
+                rhs_scale=scales[d][:, a:z],
                 start=True,
                 stop=True,
             )
 
         gate = [keep.tile([P, V], F32, name=f"gate{m}") for m in range(2)]
         result = [keep.tile([P, V], F32, name=f"result{m}") for m in range(2)]
+        y1_hi = [psum.tile([P, HALF], F32, name=f"y1_hi{m}") for m in range(2)]
+        y1_lo = [psum.tile([P, C], F32, name=f"y1_lo{m}") for m in range(2)]
+        y0_hi = [psum.tile([P, HALF], F32, name=f"y0_hi{m}") for m in range(2)]
+        y0_lo = [psum.tile([P, C], F32, name=f"y0_lo{m}") for m in range(2)]
 
         cast_w(1)
-        quantize(codes["x"], scales["x"], grouped["x"], 0, C)
-        quantize(w_codes[1], w_scales[1], w_grouped[1], 0, N)
-        y1x = [psum.tile([P, C], F32, name=f"y1x{m}") for m in range(2)]
+        quantize(1, C, V)
+        quantize_w(1)
         for m in range(2):
-            multiply(y1x[m][:], 1, m, "x", 0, C)
+            multiply(y1_hi[m][:], 1, m, C, V)
+        quantize(1, 0, C)
+        for m in range(2):
+            multiply(y1_lo[m][:], 1, m, 0, C)
         cast_w(0)
-        quantize(codes["y"], scales["y"], grouped["y"], 0, C)
-        quantize(w_codes[0], w_scales[0], w_grouped[0], 0, N)
-        y1y = [psum.tile([P, HALF], F32, name=f"y1y{m}") for m in range(2)]
-        y0y = [psum.tile([P, HALF], F32, name=f"y0y{m}") for m in range(2)]
+        quantize(0, 640, V)
+        quantize_w(0)
+        quantize(0, C, 640)
         for m in range(2):
-            multiply(y1y[m][:], 1, m, "y", HALF, C)
+            multiply(y0_hi[m][:], 0, m, C, V)
+        quantize(0, 0, C)
         for m in range(2):
-            multiply(y0y[m][:], 0, m, "y", 0, HALF)
+            multiply(y0_lo[m][:], 0, m, 0, C)
         for m in range(2):
-            nc.scalar.activation(gate[m][:, HALF:V], y1x[m][:], SIGMOID, bias=bias[m][:])
+            nc.scalar.activation(gate[m][:, C:V], y1_hi[m][:], SIGMOID, bias=bias[m][:])
         for m in range(2):
-            nc.scalar.activation(gate[m][:, 0:HALF], y1y[m][:], SIGMOID, bias=bias[m][:])
-        y0z = [psum.tile([P, C], F32, name=f"y0z{m}") for m in range(2)]
-        quantize(codes["z"], scales["z"], grouped["z"], 0, C)
-        for m in range(2):
-            multiply(y0z[m][:], 0, m, "z", 0, C)
+            nc.scalar.activation(gate[m][:, 0:C], y1_lo[m][:], SIGMOID, bias=bias[m][:])
 
         def finish(acc, m, c0, c1):
             cols = slice(c0, c1)
@@ -133,6 +152,7 @@ def tile_picked_pair_lin_gate_sub_e_kernel(tc, xT, w, b, offs, out):
             nc.sync.dma_start(out[m * M : (m + 1) * M, cols], result[m][:, cols])
 
         for m in range(2):
-            finish(y0y[m][:], m, C, V)
+            finish(y0_hi[m][:], m, C, V)
         for m in range(2):
-            finish(y0z[m][:], m, 0, C)
+            for h in range(2):
+                finish(y0_lo[m][:, h * HALF : (h + 1) * HALF], m, h * HALF, (h + 1) * HALF)

@@ -20,8 +20,10 @@ J = 4
 C = 512
 M = 128
 HALF = C // 2
+OWN = 320
+LAST = 576
 ORDER = (0, 2, 3, 1)
-CHUNKS = [[2048,2048],[2048,2048],[2048,1024,1024],[2048,1024,512,512]]
+CHUNKS = [[4096],[2048,2048],[2048,1024,1024],[2048,1024,512,512]]
 
 
 def tile_picked_pair_lin_gate_sub_e_kernel(tc, xT, w, b, offs, out):
@@ -62,7 +64,7 @@ def tile_picked_pair_lin_gate_sub_e_kernel(tc, xT, w, b, offs, out):
 
         grouped = keep.tile([P, S * J], BF16, name="grouped", align_bytes=64)
         by_entry = grouped[:].rearrange("p (n j) -> p n j", j=J)
-        tail_plain = keep.tile([P, 2, HALF], BF16, name="tail_plain")
+        tail_plain = keep.tile([P, 2, OWN], BF16, name="tail_plain")
         codes = {}
         scales = [keep.tile([P, V], U8, name=f"scales{d}", align_bytes=64) for d in range(2)]
         w_codes = [keep.tile([P, N], U32, name=f"w_codes{d}", align_bytes=64) for d in range(2)]
@@ -70,16 +72,25 @@ def tile_picked_pair_lin_gate_sub_e_kernel(tc, xT, w, b, offs, out):
 
         for step, j in enumerate(ORDER):
             for cols in spans(step):
-                nc.vector.tensor_copy(rounded[j][:, cols], planes[j][:, cols])
+                z = cols.stop - 128 if step == J - 1 and cols.stop == T else cols.stop
+                nc.vector.tensor_copy(rounded[j][:, cols.start : z], planes[j][:, cols.start : z])
+            if step == J - 1:
+                nc.scalar.copy(rounded[j][:, T - 128 :], planes[j][:, T - 128 :])
             if j < 2:
-                nc.vector.tensor_copy(tail_plain[:, j, :], planes[j][:].indirect(picks(S - HALF, S)))
-                shares = ((640, 1280), (0, 640))
+                for a in (0, OWN // 2):
+                    z = a + OWN // 2
+                    nc.vector.tensor_copy(tail_plain[:, j, a:z], planes[j][:].indirect(picks(S - OWN + a, S - OWN + z)))
+                shares = ((LAST, S - OWN), (0, LAST))
             else:
                 nc.vector.tensor_copy(by_entry[:, S - C : S, j], planes[j][:].indirect(picks(S - C, S)))
                 shares = ((C, 2 * C), (0, C))
             for a, z in shares:
                 nc.scalar.activation(by_entry[:, a:z, j], rounded[j][:].indirect(picks(a, z)), COPY)
-        nc.vector.tensor_copy(by_entry[:, S - HALF : S, 0:2], tail_plain[:].rearrange("p u n -> p n u"))
+        for a in (0, OWN // 2):
+            z = a + OWN // 2
+            nc.vector.tensor_copy(
+                by_entry[:, S - OWN + a : S - OWN + z, 0:2], tail_plain[:, :, a:z].rearrange("p u n -> p n u")
+            )
 
         w_grouped = {}
 
@@ -144,7 +155,9 @@ def tile_picked_pair_lin_gate_sub_e_kernel(tc, xT, w, b, offs, out):
         for m in range(2):
             nc.scalar.activation(gate[m][:, C:V], y1_hi[m][:], SIGMOID, bias=bias[m][:])
         for m in range(2):
-            nc.scalar.activation(gate[m][:, 0:C], y1_lo[m][:], SIGMOID, bias=bias[m][:])
+            for h in range(2):
+                cols = slice(h * HALF, (h + 1) * HALF)
+                nc.scalar.activation(gate[m][:, cols], y1_lo[m][:, cols], SIGMOID, bias=bias[m][:])
 
         def finish(acc, m, c0, c1):
             cols = slice(c0, c1)

@@ -17,13 +17,17 @@ COPY = mybir.ActivationFunctionType.Copy
 
 P = 128
 J = 4
-C = 512
 M = 128
-HALF = C // 2
+BANK = 512
+PIECE = 256
+
+ORDER = (0, 2, 3, 1)
+THIRD = S // 3
 OWN = 320
 LAST = 576
-ORDER = (0, 2, 3, 1)
-CHUNKS = [[4096],[2048,2048],[2048,1024,1024],[2048,1024,512,512]]
+EARLY = V - M
+ASSIST = 128
+LOADS = ((4096,), (2560, 1536), (2304, 1024, 768), (2048, 1024, 512, 512))
 
 
 def tile_picked_pair_lin_gate_sub_e_kernel(tc, xT, w, b, offs, out):
@@ -40,15 +44,15 @@ def tile_picked_pair_lin_gate_sub_e_kernel(tc, xT, w, b, offs, out):
         w_raw = [keep.tile([P, J, N], F32, name=f"w_raw{d}", tag=f"side{d}", align_bytes=64) for d in range(2)]
         bias = [keep.tile([P, 1], F32, name=f"bias{m}") for m in range(2)]
 
-        def spans(j):
-            edges = [sum(CHUNKS[j][:i]) for i in range(len(CHUNKS[j]) + 1)]
+        def loads(step):
+            edges = [sum(LOADS[step][:i]) for i in range(len(LOADS[step]) + 1)]
             return [slice(a, z) for a, z in zip(edges, edges[1:])]
 
         for step, j in enumerate(ORDER):
-            for i, cols in enumerate(spans(step)):
+            for cols in loads(step):
                 nc.sync.dma_start(planes[j][:, cols], x_rows[:, j, cols])
-                if (step, i) == (0, 0):
-                    nc.sync.dma_start(list_sb[:], offs)
+            if step == 0:
+                nc.sync.dma_start(list_sb[:], offs)
         for d in (1, 0):
             nc.sync.dma_start(w_raw[d][:], w[d].rearrange("(p j) n -> p j n", j=J))
         for m in range(2):
@@ -64,37 +68,38 @@ def tile_picked_pair_lin_gate_sub_e_kernel(tc, xT, w, b, offs, out):
 
         grouped = keep.tile([P, S * J], BF16, name="grouped", align_bytes=64)
         by_entry = grouped[:].rearrange("p (n j) -> p n j", j=J)
-        tail_plain = keep.tile([P, 2, OWN], BF16, name="tail_plain")
+        own_plain = keep.tile([P, 2, OWN], BF16, name="own_plain")
         codes = {}
         scales = [keep.tile([P, V], U8, name=f"scales{d}", align_bytes=64) for d in range(2)]
         w_codes = [keep.tile([P, N], U32, name=f"w_codes{d}", align_bytes=64) for d in range(2)]
         w_scales = [keep.tile([P, N], U8, name=f"w_scales{d}", align_bytes=64) for d in range(2)]
 
+        own_halves = [(a, a + OWN // 2) for a in (0, OWN // 2)]
+        own_start = S - OWN
         for step, j in enumerate(ORDER):
-            for cols in spans(step):
-                z = cols.stop - 128 if step == J - 1 and cols.stop == T else cols.stop
+            vector_stop = T - ASSIST if step == J - 1 else T
+            for cols in loads(step):
+                z = min(cols.stop, vector_stop)
                 nc.vector.tensor_copy(rounded[j][:, cols.start : z], planes[j][:, cols.start : z])
-            if step == J - 1:
-                nc.scalar.copy(rounded[j][:, T - 128 :], planes[j][:, T - 128 :])
+            if vector_stop < T:
+                nc.scalar.copy(rounded[j][:, vector_stop:], planes[j][:, vector_stop:])
             if j < 2:
-                for a in (0, OWN // 2):
-                    z = a + OWN // 2
-                    nc.vector.tensor_copy(tail_plain[:, j, a:z], planes[j][:].indirect(picks(S - OWN + a, S - OWN + z)))
-                shares = ((LAST, S - OWN), (0, LAST))
+                for a, z in own_halves:
+                    nc.vector.tensor_copy(own_plain[:, j, a:z], planes[j][:].indirect(picks(own_start + a, own_start + z)))
+                scalar_shares = ((LAST, own_start), (0, LAST))
             else:
-                nc.vector.tensor_copy(by_entry[:, S - C : S, j], planes[j][:].indirect(picks(S - C, S)))
-                shares = ((C, 2 * C), (0, C))
-            for a, z in shares:
+                nc.vector.tensor_copy(by_entry[:, 2 * THIRD : S, j], planes[j][:].indirect(picks(2 * THIRD, S)))
+                scalar_shares = ((THIRD, 2 * THIRD), (0, THIRD))
+            for a, z in scalar_shares:
                 nc.scalar.activation(by_entry[:, a:z, j], rounded[j][:].indirect(picks(a, z)), COPY)
-        for a in (0, OWN // 2):
-            z = a + OWN // 2
+        for a, z in own_halves:
             nc.vector.tensor_copy(
-                by_entry[:, S - OWN + a : S - OWN + z, 0:2], tail_plain[:, :, a:z].rearrange("p u n -> p n u")
+                by_entry[:, own_start + a : own_start + z, 0:2], own_plain[:, :, a:z].rearrange("p u n -> p n u")
             )
 
         w_grouped = {}
 
-        def cast_w(d):
+        def round_w(d):
             w_grouped[d] = keep.tile([P, N, J], BF16, name=f"w_grouped{d}", tag="w_grouped", align_bytes=64)
             nc.vector.tensor_copy(
                 w_grouped[d][:].rearrange("p (c i) j -> p c j i", i=4),
@@ -116,56 +121,47 @@ def tile_picked_pair_lin_gate_sub_e_kernel(tc, xT, w, b, offs, out):
                 in_=grouped[:, J * (d * V + a) : J * (d * V + z)],
             )
 
-        def multiply(acc, d, m, a, z):
-            cols = slice(m * M, (m + 1) * M)
-            nc.tensor.matmul_mx(
-                out=acc,
-                lhsT=w_codes[d][:, cols].bitcast(FP8X4),
-                lhsT_scale=w_scales[d][:, cols],
-                rhs=codes[d][:, a:z].bitcast(FP8X4),
-                rhs_scale=scales[d][:, a:z],
-                start=True,
-                stop=True,
-            )
+        def multiply(acc, d, a, z):
+            for m in range(2):
+                cols = slice(m * M, (m + 1) * M)
+                nc.tensor.matmul_mx(
+                    out=acc[m][:],
+                    lhsT=w_codes[d][:, cols].bitcast(FP8X4),
+                    lhsT_scale=w_scales[d][:, cols],
+                    rhs=codes[d][:, a:z].bitcast(FP8X4),
+                    rhs_scale=scales[d][:, a:z],
+                    start=True,
+                    stop=True,
+                )
 
         gate = [keep.tile([P, V], F32, name=f"gate{m}") for m in range(2)]
         result = [keep.tile([P, V], F32, name=f"result{m}") for m in range(2)]
-        y1_hi = [psum.tile([P, HALF], F32, name=f"y1_hi{m}") for m in range(2)]
-        y1_lo = [psum.tile([P, C], F32, name=f"y1_lo{m}") for m in range(2)]
-        y0_hi = [psum.tile([P, HALF], F32, name=f"y0_hi{m}") for m in range(2)]
-        y0_lo = [psum.tile([P, C], F32, name=f"y0_lo{m}") for m in range(2)]
+        y1_hi = [psum.tile([P, V - BANK], F32, name=f"y1_hi{m}") for m in range(2)]
+        y1_lo = [psum.tile([P, BANK], F32, name=f"y1_lo{m}") for m in range(2)]
+        y0_hi = [psum.tile([P, V - BANK], F32, name=f"y0_hi{m}") for m in range(2)]
+        y0_lo = [psum.tile([P, BANK], F32, name=f"y0_lo{m}") for m in range(2)]
 
-        cast_w(1)
-        quantize(1, C, V)
+        round_w(1)
+        quantize(1, BANK, V)
         quantize_w(1)
-        for m in range(2):
-            multiply(y1_hi[m][:], 1, m, C, V)
-        quantize(1, 0, C)
-        for m in range(2):
-            multiply(y1_lo[m][:], 1, m, 0, C)
-        cast_w(0)
-        quantize(0, 640, V)
+        multiply(y1_hi, 1, BANK, V)
+        quantize(1, 0, BANK)
+        multiply(y1_lo, 1, 0, BANK)
+        round_w(0)
+        quantize(0, EARLY, V)
         quantize_w(0)
-        quantize(0, C, 640)
-        for m in range(2):
-            multiply(y0_hi[m][:], 0, m, C, V)
-        quantize(0, 0, C)
-        for m in range(2):
-            multiply(y0_lo[m][:], 0, m, 0, C)
-        for m in range(2):
-            nc.scalar.activation(gate[m][:, C:V], y1_hi[m][:], SIGMOID, bias=bias[m][:])
-        for m in range(2):
-            for h in range(2):
-                cols = slice(h * HALF, (h + 1) * HALF)
-                nc.scalar.activation(gate[m][:, cols], y1_lo[m][:, cols], SIGMOID, bias=bias[m][:])
+        quantize(0, BANK, EARLY)
+        multiply(y0_hi, 0, BANK, V)
+        quantize(0, 0, BANK)
+        multiply(y0_lo, 0, 0, BANK)
 
-        def finish(acc, m, c0, c1):
-            cols = slice(c0, c1)
-            nc.vector.tensor_tensor(result[m][:, cols], acc, gate[m][:, cols], MULT)
+        pieces = [(m, BANK, y1_hi[m][:], y0_hi[m][:]) for m in range(2)]
+        pieces = pieces + [
+            (m, a, y1_lo[m][:, a : a + PIECE], y0_lo[m][:, a : a + PIECE]) for m in range(2) for a in (0, PIECE)
+        ]
+        for m, a, y1, y0 in pieces:
+            nc.scalar.activation(gate[m][:, a : a + PIECE], y1, SIGMOID, bias=bias[m][:])
+        for m, a, y1, y0 in pieces:
+            cols = slice(a, a + PIECE)
+            nc.vector.tensor_tensor(result[m][:, cols], y0, gate[m][:, cols], MULT)
             nc.sync.dma_start(out[m * M : (m + 1) * M, cols], result[m][:, cols])
-
-        for m in range(2):
-            finish(y0_hi[m][:], m, C, V)
-        for m in range(2):
-            for h in range(2):
-                finish(y0_lo[m][:, h * HALF : (h + 1) * HALF], m, h * HALF, (h + 1) * HALF)

@@ -26,8 +26,8 @@ THIRD = S // 3
 OWN = 320
 LAST = 576
 EARLY = V - M
-ASSIST = 128
-LOADS = ((4096,), (2560, 1536), (2304, 1024, 768), (2048, 1024, 512, 512))
+LOADS = ((4096,), (4096,), (2688, 1408), (2368, 1152, 576))
+ASSIST = (1344, 1344, 0, 176)
 
 
 def tile_picked_pair_lin_gate_sub_e_kernel(tc, xT, w, b, offs, out):
@@ -68,7 +68,7 @@ def tile_picked_pair_lin_gate_sub_e_kernel(tc, xT, w, b, offs, out):
 
         grouped = keep.tile([P, S * J], BF16, name="grouped", align_bytes=64)
         by_entry = grouped[:].rearrange("p (n j) -> p n j", j=J)
-        own_plain = keep.tile([P, 2, OWN], BF16, name="own_plain")
+        own_plain = keep.tile([P, OWN], BF16, name="own_plain")
         codes = {}
         scales = [keep.tile([P, V], U8, name=f"scales{d}", align_bytes=64) for d in range(2)]
         w_codes = [keep.tile([P, N], U32, name=f"w_codes{d}", align_bytes=64) for d in range(2)]
@@ -77,25 +77,26 @@ def tile_picked_pair_lin_gate_sub_e_kernel(tc, xT, w, b, offs, out):
         own_halves = [(a, a + OWN // 2) for a in (0, OWN // 2)]
         own_start = S - OWN
         for step, j in enumerate(ORDER):
-            vector_stop = T - ASSIST if step == J - 1 else T
+            vector_stop = T - ASSIST[step]
             for cols in loads(step):
                 z = min(cols.stop, vector_stop)
                 nc.vector.tensor_copy(rounded[j][:, cols.start : z], planes[j][:, cols.start : z])
             if vector_stop < T:
                 nc.scalar.copy(rounded[j][:, vector_stop:], planes[j][:, vector_stop:])
-            if j < 2:
+            if step == J - 1:
                 for a, z in own_halves:
-                    nc.vector.tensor_copy(own_plain[:, j, a:z], planes[j][:].indirect(picks(own_start + a, own_start + z)))
+                    nc.vector.tensor_copy(own_plain[:, a:z], planes[j][:].indirect(picks(own_start + a, own_start + z)))
                 scalar_shares = ((LAST, own_start), (0, LAST))
+            elif step == 0:
+                nc.vector.tensor_copy(by_entry[:, V:S, j], planes[j][:].indirect(picks(V, S)))
+                scalar_shares = ((0, V),)
             else:
                 nc.vector.tensor_copy(by_entry[:, 2 * THIRD : S, j], planes[j][:].indirect(picks(2 * THIRD, S)))
-                scalar_shares = ((THIRD, 2 * THIRD), (0, THIRD))
+                scalar_shares = ((0, 2 * THIRD),)
             for a, z in scalar_shares:
                 nc.scalar.activation(by_entry[:, a:z, j], rounded[j][:].indirect(picks(a, z)), COPY)
         for a, z in own_halves:
-            nc.vector.tensor_copy(
-                by_entry[:, own_start + a : own_start + z, 0:2], own_plain[:, :, a:z].rearrange("p u n -> p n u")
-            )
+            nc.vector.tensor_copy(by_entry[:, own_start + a : own_start + z, ORDER[-1]], own_plain[:, a:z])
 
         w_grouped = {}
 

@@ -21,13 +21,11 @@ M = 128
 BANK = 512
 PIECE = 256
 
-ORDER = (0, 2, 3, 1)
-THIRD = S // 3
-OWN = 320
+OWN = (512, 512, 512, 320)
 LAST = 576
 EARLY = V - M
-LOADS = ((4096,), (4096,), (2688, 1408), (2368, 1152, 576))
-ASSIST = (1344, 1344, 0, 176)
+LOADS = ((4096,), (2816, 1280), (2816, 1280), (2304, 1152, 640))
+ASSIST = (1344, 384, 768, 192)
 
 
 def tile_picked_pair_lin_gate_sub_e_kernel(tc, xT, w, b, offs, out):
@@ -44,14 +42,14 @@ def tile_picked_pair_lin_gate_sub_e_kernel(tc, xT, w, b, offs, out):
         w_raw = [keep.tile([P, J, N], F32, name=f"w_raw{d}", tag=f"side{d}", align_bytes=64) for d in range(2)]
         bias = [keep.tile([P, 1], F32, name=f"bias{m}") for m in range(2)]
 
-        def loads(step):
-            edges = [sum(LOADS[step][:i]) for i in range(len(LOADS[step]) + 1)]
+        def loads(j):
+            edges = [sum(LOADS[j][:i]) for i in range(len(LOADS[j]) + 1)]
             return [slice(a, z) for a, z in zip(edges, edges[1:])]
 
-        for step, j in enumerate(ORDER):
-            for cols in loads(step):
+        for j in range(J):
+            for cols in loads(j):
                 nc.sync.dma_start(planes[j][:, cols], x_rows[:, j, cols])
-            if step == 0:
+            if j == 0:
                 nc.sync.dma_start(list_sb[:], offs)
         for d in (1, 0):
             nc.sync.dma_start(w_raw[d][:], w[d].rearrange("(p j) n -> p j n", j=J))
@@ -68,36 +66,33 @@ def tile_picked_pair_lin_gate_sub_e_kernel(tc, xT, w, b, offs, out):
 
         grouped = keep.tile([P, S * J], BF16, name="grouped", align_bytes=64)
         by_entry = grouped[:].rearrange("p (n j) -> p n j", j=J)
-        own_plain = keep.tile([P, OWN], BF16, name="own_plain")
+        own_plain = keep.tile([P, OWN[-1]], BF16, name="own_plain")
+
+        for j in range(J):
+            vector_stop = T - ASSIST[j]
+            for cols in loads(j):
+                z = min(cols.stop, vector_stop)
+                if cols.start < z:
+                    nc.vector.tensor_copy(rounded[j][:, cols.start : z], planes[j][:, cols.start : z])
+            if vector_stop < T:
+                nc.scalar.copy(rounded[j][:, vector_stop:], planes[j][:, vector_stop:])
+            first = S - OWN[j]
+            if j < J - 1:
+                nc.vector.tensor_copy(by_entry[:, first:S, j], planes[j][:].indirect(picks(first, S)))
+                nc.scalar.activation(by_entry[:, 0:first, j], rounded[j][:].indirect(picks(0, first)), COPY)
+            else:
+                halves = [(a, a + OWN[j] // 2) for a in (0, OWN[j] // 2)]
+                for a, z in halves:
+                    nc.vector.tensor_copy(own_plain[:, a:z], planes[j][:].indirect(picks(first + a, first + z)))
+                for a, z in ((LAST, first), (0, LAST)):
+                    nc.scalar.activation(by_entry[:, a:z, j], rounded[j][:].indirect(picks(a, z)), COPY)
+                for a, z in halves:
+                    nc.vector.tensor_copy(by_entry[:, first + a : first + z, j], own_plain[:, a:z])
+
         codes = {}
         scales = [keep.tile([P, V], U8, name=f"scales{d}", align_bytes=64) for d in range(2)]
         w_codes = [keep.tile([P, N], U32, name=f"w_codes{d}", align_bytes=64) for d in range(2)]
         w_scales = [keep.tile([P, N], U8, name=f"w_scales{d}", align_bytes=64) for d in range(2)]
-
-        own_halves = [(a, a + OWN // 2) for a in (0, OWN // 2)]
-        own_start = S - OWN
-        for step, j in enumerate(ORDER):
-            vector_stop = T - ASSIST[step]
-            for cols in loads(step):
-                z = min(cols.stop, vector_stop)
-                nc.vector.tensor_copy(rounded[j][:, cols.start : z], planes[j][:, cols.start : z])
-            if vector_stop < T:
-                nc.scalar.copy(rounded[j][:, vector_stop:], planes[j][:, vector_stop:])
-            if step == J - 1:
-                for a, z in own_halves:
-                    nc.vector.tensor_copy(own_plain[:, a:z], planes[j][:].indirect(picks(own_start + a, own_start + z)))
-                scalar_shares = ((LAST, own_start), (0, LAST))
-            elif step == 0:
-                nc.vector.tensor_copy(by_entry[:, V:S, j], planes[j][:].indirect(picks(V, S)))
-                scalar_shares = ((0, V),)
-            else:
-                nc.vector.tensor_copy(by_entry[:, 2 * THIRD : S, j], planes[j][:].indirect(picks(2 * THIRD, S)))
-                scalar_shares = ((0, 2 * THIRD),)
-            for a, z in scalar_shares:
-                nc.scalar.activation(by_entry[:, a:z, j], rounded[j][:].indirect(picks(a, z)), COPY)
-        for a, z in own_halves:
-            nc.vector.tensor_copy(by_entry[:, own_start + a : own_start + z, ORDER[-1]], own_plain[:, a:z])
-
         w_grouped = {}
 
         def round_w(d):

@@ -24,8 +24,8 @@ PIECE = 256
 OWN = (512, 512, 512, 320)
 LAST = 576
 EARLY = V - M
-LOADS = ((4096,), (2816, 1280), (2816, 1280), (2304, 1152, 640))
-ASSIST = (1344, 384, 768, 192)
+LOADS = ((2816, 1280), (2560, 1536), (2304, 1024, 768), (2304, 1152, 640))
+ASSIST = (384, 384, 0, 192)
 
 
 def tile_picked_pair_lin_gate_sub_e_kernel(tc, xT, w, b, offs, out):

@@ -21,11 +21,10 @@ M = 128
 BANK = 512
 PIECE = 256
 
-OWN = (512, 512, 512, 320)
-LAST = 576
-EARLY = V - M
-LOADS = ((2816, 1280), (2560, 1536), (2304, 1024, 768), (2304, 1152, 640))
-ASSIST = (384, 384, 0, 192)
+OWN = (512, 512, 512, 384)
+LAST = 512
+LOADS = ((2816, 1280), (2560, 1536), (2304, 1024, 768), (2176, 1088, 576, 256))
+ASSIST = (384, 384, 0, 256)
 
 
 def tile_picked_pair_lin_gate_sub_e_kernel(tc, xT, w, b, offs, out):
@@ -117,47 +116,47 @@ def tile_picked_pair_lin_gate_sub_e_kernel(tc, xT, w, b, offs, out):
                 in_=grouped[:, J * (d * V + a) : J * (d * V + z)],
             )
 
-        def multiply(acc, d, a, z):
-            for m in range(2):
-                cols = slice(m * M, (m + 1) * M)
-                nc.tensor.matmul_mx(
-                    out=acc[m][:],
-                    lhsT=w_codes[d][:, cols].bitcast(FP8X4),
-                    lhsT_scale=w_scales[d][:, cols],
-                    rhs=codes[d][:, a:z].bitcast(FP8X4),
-                    rhs_scale=scales[d][:, a:z],
-                    start=True,
-                    stop=True,
-                )
+        def multiply(acc, d, m, a, z):
+            cols = slice(m * M, (m + 1) * M)
+            nc.tensor.matmul_mx(
+                out=acc,
+                lhsT=w_codes[d][:, cols].bitcast(FP8X4),
+                lhsT_scale=w_scales[d][:, cols],
+                rhs=codes[d][:, a:z].bitcast(FP8X4),
+                rhs_scale=scales[d][:, a:z],
+                start=True,
+                stop=True,
+            )
 
         gate = [keep.tile([P, V], F32, name=f"gate{m}") for m in range(2)]
         result = [keep.tile([P, V], F32, name=f"result{m}") for m in range(2)]
-        y1_hi = [psum.tile([P, V - BANK], F32, name=f"y1_hi{m}") for m in range(2)]
-        y1_lo = [psum.tile([P, BANK], F32, name=f"y1_lo{m}") for m in range(2)]
-        y0_hi = [psum.tile([P, V - BANK], F32, name=f"y0_hi{m}") for m in range(2)]
-        y0_lo = [psum.tile([P, BANK], F32, name=f"y0_lo{m}") for m in range(2)]
+        y = {}
+
+        def products(d, a):
+            for m in range(2):
+                y[d, m, a] = psum.tile([P, PIECE], F32, name=f"y{d}_{m}_{a}", tag=f"bank_{m}_{a}")[:]
+                multiply(y[d, m, a], d, m, a, a + PIECE)
 
         round_w(1)
         quantize(1, BANK, V)
         quantize_w(1)
-        multiply(y1_hi, 1, BANK, V)
+        products(1, BANK)
         quantize(1, 0, BANK)
-        multiply(y1_lo, 1, 0, BANK)
+        products(1, PIECE)
+        products(1, 0)
+        for a in (BANK, PIECE, 0):
+            for m in range(2):
+                nc.scalar.activation(gate[m][:, a : a + PIECE], y[1, m, a], SIGMOID, bias=bias[m][:])
         round_w(0)
-        quantize(0, EARLY, V)
+        quantize(0, BANK, V)
         quantize_w(0)
-        quantize(0, BANK, EARLY)
-        multiply(y0_hi, 0, BANK, V)
-        quantize(0, 0, BANK)
-        multiply(y0_lo, 0, 0, BANK)
+        products(0, BANK)
+        for a in (PIECE, 0):
+            quantize(0, a, a + PIECE)
+            products(0, a)
 
-        pieces = [(m, BANK, y1_hi[m][:], y0_hi[m][:]) for m in range(2)]
-        pieces = pieces + [
-            (m, a, y1_lo[m][:, a : a + PIECE], y0_lo[m][:, a : a + PIECE]) for m in range(2) for a in (0, PIECE)
-        ]
-        for m, a, y1, y0 in pieces:
-            nc.scalar.activation(gate[m][:, a : a + PIECE], y1, SIGMOID, bias=bias[m][:])
-        for m, a, y1, y0 in pieces:
+        for a in (BANK, PIECE, 0):
             cols = slice(a, a + PIECE)
-            nc.vector.tensor_tensor(result[m][:, cols], y0, gate[m][:, cols], MULT)
-            nc.sync.dma_start(out[m * M : (m + 1) * M, cols], result[m][:, cols])
+            for m in range(2):
+                nc.vector.tensor_tensor(result[m][:, cols], y[0, m, a], gate[m][:, cols], MULT)
+                nc.sync.dma_start(out[m * M : (m + 1) * M, cols], result[m][:, cols])

@@ -18,11 +18,9 @@ COPY = mybir.ActivationFunctionType.Copy
 P = 128
 J = 4
 M = 128
-BANK = 512
 PIECE = 256
-
-OWN = (512, 512, 512, 384)
-LAST = 512
+SPLIT = 1024
+THIRD = S // 3
 LOADS = ((2816, 1280), (2560, 1536), (2304, 1024, 768), (2176, 1088, 576, 256))
 ASSIST = (384, 384, 0, 256)
 
@@ -38,7 +36,8 @@ def tile_picked_pair_lin_gate_sub_e_kernel(tc, xT, w, b, offs, out):
         list_sb = keep.tile([P, S // 16], U16, name="list_sb")
         planes = [keep.tile([P, T], F32, name=f"plane{j}") for j in range(J)]
         rounded = [keep.tile([P, T], BF16, name=f"rounded{j}") for j in range(J)]
-        w_raw = [keep.tile([P, J, N], F32, name=f"w_raw{d}", tag=f"side{d}", align_bytes=64) for d in range(2)]
+        raw_w1 = keep.tile([P, J, N], F32, name="raw_w1", tag="w_raw1", align_bytes=64)
+        raw_w0 = [keep.tile([P, J, M], F32, name=f"raw_w0{m}", tag=f"w_raw0{m}", align_bytes=64) for m in range(2)]
         bias = [keep.tile([P, 1], F32, name=f"bias{m}") for m in range(2)]
 
         def loads(j):
@@ -50,8 +49,9 @@ def tile_picked_pair_lin_gate_sub_e_kernel(tc, xT, w, b, offs, out):
                 nc.sync.dma_start(planes[j][:, cols], x_rows[:, j, cols])
             if j == 0:
                 nc.sync.dma_start(list_sb[:], offs)
-        for d in (1, 0):
-            nc.sync.dma_start(w_raw[d][:], w[d].rearrange("(p j) n -> p j n", j=J))
+        nc.sync.dma_start(raw_w1[:], w[1].rearrange("(p j) n -> p j n", j=J))
+        for m in range(2):
+            nc.sync.dma_start(raw_w0[m][:], w[0].rearrange("(p j) n -> p j n", j=J)[:, :, m * M : (m + 1) * M])
         for m in range(2):
             nc.sync.dma_start(bias[m][:], b[m * M : (m + 1) * M, :])
 
@@ -60,12 +60,30 @@ def tile_picked_pair_lin_gate_sub_e_kernel(tc, xT, w, b, offs, out):
         nc.vector.memset(warm[:], 0.0)
         nc.scalar.activation(warm_out[:], warm[:], SIGMOID)
 
+        w_codes = {}
+        w_scales = [keep.tile([P, N], U8, name=f"w_scales{d}", align_bytes=64) for d in range(2)]
+
+        def round_w(copy, grouped_w, raw):
+            copy(
+                grouped_w[:].rearrange("p (c i) j -> p c j i", i=4),
+                raw[:].rearrange("p j (c i) -> p c j i", i=4),
+            )
+
+        def quantize_w(d, grouped_w, cols, tag):
+            made = keep.tile([P, cols.stop - cols.start], U32, name=f"w_codes{d}_{cols.start}", tag=tag, align_bytes=64)
+            for a in range(cols.start, cols.stop, M):
+                w_codes[d, a // M] = made[:, a - cols.start : a - cols.start + M].bitcast(FP8X4)
+            nc.vector.quantize_mx(
+                out=made[:].bitcast(FP8X4),
+                scales=w_scales[d][:, cols],
+                in_=grouped_w[:].rearrange("p n j -> p (n j)"),
+            )
+
         def picks(a, z):
             return list_sb[:, a // 16 : z // 16]
 
         grouped = keep.tile([P, S * J], BF16, name="grouped", align_bytes=64)
         by_entry = grouped[:].rearrange("p (n j) -> p n j", j=J)
-        own_plain = keep.tile([P, OWN[-1]], BF16, name="own_plain")
 
         for j in range(J):
             vector_stop = T - ASSIST[j]
@@ -75,88 +93,76 @@ def tile_picked_pair_lin_gate_sub_e_kernel(tc, xT, w, b, offs, out):
                     nc.vector.tensor_copy(rounded[j][:, cols.start : z], planes[j][:, cols.start : z])
             if vector_stop < T:
                 nc.scalar.copy(rounded[j][:, vector_stop:], planes[j][:, vector_stop:])
-            first = S - OWN[j]
-            if j < J - 1:
-                nc.vector.tensor_copy(by_entry[:, first:S, j], planes[j][:].indirect(picks(first, S)))
-                nc.scalar.activation(by_entry[:, 0:first, j], rounded[j][:].indirect(picks(0, first)), COPY)
-            else:
-                halves = [(a, a + OWN[j] // 2) for a in (0, OWN[j] // 2)]
-                for a, z in halves:
-                    nc.vector.tensor_copy(own_plain[:, a:z], planes[j][:].indirect(picks(first + a, first + z)))
-                for a, z in ((LAST, first), (0, LAST)):
-                    nc.scalar.activation(by_entry[:, a:z, j], rounded[j][:].indirect(picks(a, z)), COPY)
-                for a, z in halves:
-                    nc.vector.tensor_copy(by_entry[:, first + a : first + z, j], own_plain[:, a:z])
+            nc.vector.tensor_copy(by_entry[:, 2 * THIRD : S, j], planes[j][:].indirect(picks(2 * THIRD, S)))
+            shares = ((0, 2 * THIRD),) if j < J - 1 else ((THIRD, 2 * THIRD), (0, THIRD))
+            for a, z in shares:
+                nc.scalar.activation(by_entry[:, a:z, j], rounded[j][:].indirect(picks(a, z)), COPY)
 
-        codes = {}
-        scales = [keep.tile([P, V], U8, name=f"scales{d}", align_bytes=64) for d in range(2)]
-        w_codes = [keep.tile([P, N], U32, name=f"w_codes{d}", align_bytes=64) for d in range(2)]
-        w_scales = [keep.tile([P, N], U8, name=f"w_scales{d}", align_bytes=64) for d in range(2)]
-        w_grouped = {}
-
-        def round_w(d):
-            w_grouped[d] = keep.tile([P, N, J], BF16, name=f"w_grouped{d}", tag="w_grouped", align_bytes=64)
-            nc.vector.tensor_copy(
-                w_grouped[d][:].rearrange("p (c i) j -> p c j i", i=4),
-                w_raw[d][:].rearrange("p j (c i) -> p c j i", i=4),
-            )
-            codes[d] = keep.tile([P, V], U32, name=f"codes{d}", tag=f"side{d}", align_bytes=64)
-
-        def quantize_w(d):
-            nc.vector.quantize_mx(
-                out=w_codes[d][:].bitcast(FP8X4),
-                scales=w_scales[d][:],
-                in_=w_grouped[d][:].rearrange("p n j -> p (n j)"),
-            )
-
-        def quantize(d, a, z):
-            nc.vector.quantize_mx(
-                out=codes[d][:, a:z].bitcast(FP8X4),
-                scales=scales[d][:, a:z],
-                in_=grouped[:, J * (d * V + a) : J * (d * V + z)],
-            )
-
-        def multiply(acc, d, m, a, z):
-            cols = slice(m * M, (m + 1) * M)
-            nc.tensor.matmul_mx(
-                out=acc,
-                lhsT=w_codes[d][:, cols].bitcast(FP8X4),
-                lhsT_scale=w_scales[d][:, cols],
-                rhs=codes[d][:, a:z].bitcast(FP8X4),
-                rhs_scale=scales[d][:, a:z],
-                start=True,
-                stop=True,
-            )
-
+        scales = keep.tile([P, S], U8, name="scales", align_bytes=64)
         gate = [keep.tile([P, V], F32, name=f"gate{m}") for m in range(2)]
         result = [keep.tile([P, V], F32, name=f"result{m}") for m in range(2)]
         y = {}
 
-        def products(d, a):
-            for m in range(2):
-                y[d, m, a] = psum.tile([P, PIECE], F32, name=f"y{d}_{m}_{a}", tag=f"bank_{m}_{a}")[:]
-                multiply(y[d, m, a], d, m, a, a + PIECE)
+        codes = {}
 
-        round_w(1)
-        quantize(1, BANK, V)
-        quantize_w(1)
-        products(1, BANK)
-        quantize(1, 0, BANK)
-        products(1, PIECE)
-        products(1, 0)
-        for a in (BANK, PIECE, 0):
-            for m in range(2):
-                nc.scalar.activation(gate[m][:, a : a + PIECE], y[1, m, a], SIGMOID, bias=bias[m][:])
-        round_w(0)
-        quantize(0, BANK, V)
-        quantize_w(0)
-        products(0, BANK)
-        for a in (PIECE, 0):
-            quantize(0, a, a + PIECE)
-            products(0, a)
+        def words(a, z):
+            return codes[a // SPLIT][:, a % SPLIT : a % SPLIT + z - a].bitcast(FP8X4)
 
-        for a in (BANK, PIECE, 0):
-            cols = slice(a, a + PIECE)
-            for m in range(2):
+        def quantize(a, z):
+            nc.vector.quantize_mx(out=words(a, z), scales=scales[:, a:z], in_=grouped[:, J * a : J * z])
+
+        def product(d, m, a, bank):
+            first = d * V + a
+            cols = slice(m * M, (m + 1) * M)
+            y[d, m, a] = psum.tile([P, PIECE], F32, name=f"y{d}_{m}_{a}", tag=f"bank{bank}")[:]
+            nc.tensor.matmul_mx(
+                out=y[d, m, a],
+                lhsT=w_codes[d, m],
+                lhsT_scale=w_scales[d][:, cols],
+                rhs=words(first, first + PIECE),
+                rhs_scale=scales[:, first : first + PIECE],
+                start=True,
+                stop=True,
+            )
+
+        def sigmoid(m, a):
+            nc.scalar.activation(gate[m][:, a : a + PIECE], y[1, m, a], SIGMOID, bias=bias[m][:])
+
+        hi, mid, lo = 2 * PIECE, PIECE, 0
+        halves = (slice(0, M), slice(M, N))
+        grouped_w1 = keep.tile([P, N, J], BF16, name="grouped_w1", tag="grouped_w", align_bytes=64)
+        round_w(nc.vector.tensor_copy, grouped_w1, raw_w1)
+        codes[1] = keep.tile([P, SPLIT], U32, name="codes_hi", tag="w_raw1", align_bytes=64)
+        quantize(V + hi, S)
+        quantize_w(1, grouped_w1, slice(0, N), "w_codes1")
+        product(1, 0, hi, 0)
+        quantize(V + mid, V + hi)
+        product(1, 0, mid, 1)
+        product(1, 1, hi, 3)
+        product(1, 1, mid, 4)
+        grouped_w0a = keep.tile([P, M, J], BF16, name="grouped_w0a", tag="grouped_w", align_bytes=64)
+        grouped_w0b = keep.tile([P, M, J], BF16, name="grouped_w0b", align_bytes=64)
+        round_w(nc.vector.tensor_copy, grouped_w0a, raw_w0[0])
+        round_w(nc.scalar.copy, grouped_w0b, raw_w0[1])
+        codes[0] = keep.tile([P, SPLIT], U32, name="codes_lo", tag="w_raw00", align_bytes=64)
+        quantize(hi, V + mid)
+        quantize_w(0, grouped_w0a, halves[0], "w_codes0")
+        product(0, 0, hi, 6)
+        product(1, 0, lo, 2)
+        product(1, 1, lo, 5)
+        for m in range(2):
+            for a in (hi, mid, lo):
+                sigmoid(m, a)
+        quantize(mid, hi)
+        product(0, 0, mid, 7)
+        quantize(lo, mid)
+        product(0, 0, lo, 0)
+        quantize_w(0, grouped_w0b, halves[1], "grouped_w")
+        for i, a in enumerate((hi, mid, lo)):
+            product(0, 1, a, (1, 2, 3)[i])
+
+        for m in range(2):
+            for a in (hi, mid, lo):
+                cols = slice(a, a + PIECE)
                 nc.vector.tensor_tensor(result[m][:, cols], y[0, m, a], gate[m][:, cols], MULT)
                 nc.sync.dma_start(out[m * M : (m + 1) * M, cols], result[m][:, cols])

@@ -19,7 +19,6 @@ P = 128
 J = 4
 M = 128
 PIECE = 256
-SPLIT = 1024
 THIRD = S // 3
 LOADS = ((2816, 1280), (2560, 1536), (2304, 1024, 768), (2176, 1088, 576, 256))
 ASSIST = (384, 384, 0, 256)
@@ -106,7 +105,7 @@ def tile_picked_pair_lin_gate_sub_e_kernel(tc, xT, w, b, offs, out):
         codes = {}
 
         def words(a, z):
-            return codes[a // SPLIT][:, a % SPLIT : a % SPLIT + z - a].bitcast(FP8X4)
+            return codes[a // V][:, a % V : a % V + z - a].bitcast(FP8X4)
 
         def quantize(a, z):
             nc.vector.quantize_mx(out=words(a, z), scales=scales[:, a:z], in_=grouped[:, J * a : J * z])
@@ -132,24 +131,25 @@ def tile_picked_pair_lin_gate_sub_e_kernel(tc, xT, w, b, offs, out):
         halves = (slice(0, M), slice(M, N))
         grouped_w1 = keep.tile([P, N, J], BF16, name="grouped_w1", tag="grouped_w", align_bytes=64)
         round_w(nc.vector.tensor_copy, grouped_w1, raw_w1)
-        codes[1] = keep.tile([P, SPLIT], U32, name="codes_hi", tag="w_raw1", align_bytes=64)
+        codes[1] = keep.tile([P, V], U32, name="codes_hi", tag="w_raw1", align_bytes=64)
         quantize(V + hi, S)
         quantize_w(1, grouped_w1, slice(0, N), "w_codes1")
         product(1, 0, hi, 0)
+        product(1, 1, hi, 3)
         quantize(V + mid, V + hi)
         product(1, 0, mid, 1)
-        product(1, 1, hi, 3)
         product(1, 1, mid, 4)
+        quantize(V + lo, V + mid)
+        product(1, 0, lo, 2)
+        product(1, 1, lo, 5)
         grouped_w0a = keep.tile([P, M, J], BF16, name="grouped_w0a", tag="grouped_w", align_bytes=64)
         grouped_w0b = keep.tile([P, M, J], BF16, name="grouped_w0b", align_bytes=64)
         round_w(nc.vector.tensor_copy, grouped_w0a, raw_w0[0])
         round_w(nc.scalar.copy, grouped_w0b, raw_w0[1])
-        codes[0] = keep.tile([P, SPLIT], U32, name="codes_lo", tag="w_raw00", align_bytes=64)
-        quantize(hi, V + mid)
+        codes[0] = keep.tile([P, V], U32, name="codes_lo", tag="w_raw00", align_bytes=64)
+        quantize(hi, V)
         quantize_w(0, grouped_w0a, halves[0], "w_codes0")
         product(0, 0, hi, 6)
-        product(1, 0, lo, 2)
-        product(1, 1, lo, 5)
         for m in range(2):
             for a in (hi, mid, lo):
                 sigmoid(m, a)

@@ -12,6 +12,7 @@ U32 = mybir.dt.uint32
 U8 = mybir.dt.uint8
 FP8X4 = mybir.dt.float8_e4m3fn_x4
 MULT = mybir.AluOpType.mult
+ADD = mybir.AluOpType.add
 SIGMOID = mybir.ActivationFunctionType.Sigmoid
 COPY = mybir.ActivationFunctionType.Copy
 
@@ -20,8 +21,8 @@ J = 4
 M = 128
 PIECE = 256
 THIRD = S // 3
-LOADS = ((2816, 1280), (2560, 1536), (2304, 1024, 768), (2176, 1088, 576, 256))
-ASSIST = (384, 384, 0, 256)
+LOADS = ((2816, 1280), (2560, 1536), (2304, 1024, 768), (2112, 1056, 544, 256, 128))
+ASSIST = (384, 384, 0, 128)
 
 
 def tile_picked_pair_lin_gate_sub_e_kernel(tc, xT, w, b, offs, out):
@@ -35,9 +36,12 @@ def tile_picked_pair_lin_gate_sub_e_kernel(tc, xT, w, b, offs, out):
         list_sb = keep.tile([P, S // 16], U16, name="list_sb")
         planes = [keep.tile([P, T], F32, name=f"plane{j}") for j in range(J)]
         rounded = [keep.tile([P, T], BF16, name=f"rounded{j}") for j in range(J)]
-        raw_w1 = keep.tile([P, J, N], F32, name="raw_w1", tag="w_raw1", align_bytes=64)
-        raw_w0 = [keep.tile([P, J, M], F32, name=f"raw_w0{m}", tag=f"w_raw0{m}", align_bytes=64) for m in range(2)]
-        bias = [keep.tile([P, 1], F32, name=f"bias{m}") for m in range(2)]
+        raw = {
+            (d, m): keep.tile([P, J, M], F32, name=f"raw{d}{m}", tag=f"raw{d}{m}", align_bytes=64)
+            for d in range(2)
+            for m in range(2)
+        }
+        bias = keep.tile([P, 2, 1], F32, name="bias")
 
         def loads(j):
             edges = [sum(LOADS[j][:i]) for i in range(len(LOADS[j]) + 1)]
@@ -48,11 +52,11 @@ def tile_picked_pair_lin_gate_sub_e_kernel(tc, xT, w, b, offs, out):
                 nc.sync.dma_start(planes[j][:, cols], x_rows[:, j, cols])
             if j == 0:
                 nc.sync.dma_start(list_sb[:], offs)
-        nc.sync.dma_start(raw_w1[:], w[1].rearrange("(p j) n -> p j n", j=J))
-        for m in range(2):
-            nc.sync.dma_start(raw_w0[m][:], w[0].rearrange("(p j) n -> p j n", j=J)[:, :, m * M : (m + 1) * M])
-        for m in range(2):
-            nc.sync.dma_start(bias[m][:], b[m * M : (m + 1) * M, :])
+        for d in (1, 0):
+            for m in range(2):
+                nc.sync.dma_start(raw[d, m][:], w[d].rearrange("(p j) n -> p j n", j=J)[:, :, m * M : (m + 1) * M])
+        with nc.allow_non_contiguous_dma(reason="one bias value a partition for each half of the channels"):
+            nc.sync.dma_start(bias[:], b.rearrange("(m p) o -> p m o", p=P))
 
         warm = keep.tile([P, 1], F32, name="warm")
         warm_out = keep.tile([P, 1], F32, name="warm_out")
@@ -62,10 +66,10 @@ def tile_picked_pair_lin_gate_sub_e_kernel(tc, xT, w, b, offs, out):
         w_codes = {}
         w_scales = [keep.tile([P, N], U8, name=f"w_scales{d}", align_bytes=64) for d in range(2)]
 
-        def round_w(copy, grouped_w, raw):
+        def round_w(copy, grouped_w, rows):
             copy(
-                grouped_w[:].rearrange("p (c i) j -> p c j i", i=4),
-                raw[:].rearrange("p j (c i) -> p c j i", i=4),
+                grouped_w.rearrange("p (c i) j -> p c j i", i=4),
+                rows[:].rearrange("p j (c i) -> p c j i", i=4),
             )
 
         def quantize_w(d, grouped_w, cols, tag):
@@ -125,13 +129,16 @@ def tile_picked_pair_lin_gate_sub_e_kernel(tc, xT, w, b, offs, out):
             )
 
         def sigmoid(m, a):
-            nc.scalar.activation(gate[m][:, a : a + PIECE], y[1, m, a], SIGMOID, bias=bias[m][:])
+            nc.scalar.activation(gate[m][:, a : a + PIECE], y[1, m, a], SIGMOID, bias=bias[:, m, :])
 
         hi, mid, lo = 2 * PIECE, PIECE, 0
         halves = (slice(0, M), slice(M, N))
         grouped_w1 = keep.tile([P, N, J], BF16, name="grouped_w1", tag="grouped_w", align_bytes=64)
-        round_w(nc.vector.tensor_copy, grouped_w1, raw_w1)
-        codes[1] = keep.tile([P, V], U32, name="codes_hi", tag="w_raw1", align_bytes=64)
+        nc.gpsimd.tensor_scalar(
+            grouped_w1[:, halves[0], :], raw[1, 0][:].rearrange("p j n -> p n j"), 1.0, 0.0, MULT, ADD
+        )
+        round_w(nc.vector.tensor_copy, grouped_w1[:, halves[1], :], raw[1, 1])
+        codes[1] = keep.tile([P, V], U32, name="codes_hi", tag="raw11", align_bytes=64)
         quantize(V + hi, S)
         quantize_w(1, grouped_w1, slice(0, N), "w_codes1")
         product(1, 0, hi, 0)
@@ -144,9 +151,9 @@ def tile_picked_pair_lin_gate_sub_e_kernel(tc, xT, w, b, offs, out):
         product(1, 1, lo, 5)
         grouped_w0a = keep.tile([P, M, J], BF16, name="grouped_w0a", tag="grouped_w", align_bytes=64)
         grouped_w0b = keep.tile([P, M, J], BF16, name="grouped_w0b", align_bytes=64)
-        round_w(nc.vector.tensor_copy, grouped_w0a, raw_w0[0])
-        round_w(nc.scalar.copy, grouped_w0b, raw_w0[1])
-        codes[0] = keep.tile([P, V], U32, name="codes_lo", tag="w_raw00", align_bytes=64)
+        round_w(nc.vector.tensor_copy, grouped_w0a[:], raw[0, 0])
+        round_w(nc.scalar.copy, grouped_w0b[:], raw[0, 1])
+        codes[0] = keep.tile([P, V], U32, name="codes_lo", tag="raw00", align_bytes=64)
         quantize(hi, V)
         quantize_w(0, grouped_w0a, halves[0], "w_codes0")
         product(0, 0, hi, 6)

@@ -106,10 +106,8 @@ def tile_picked_pair_lin_gate_sub_e_kernel(tc, xT, w, b, offs, out):
         result = [keep.tile([P, V], F32, name=f"result{m}") for m in range(2)]
         y = {}
 
-        codes = {}
-
         def words(a, z):
-            return codes[a // V][:, a % V : a % V + z - a].bitcast(FP8X4)
+            return codes[:, a:z].bitcast(FP8X4)
 
         def quantize(a, z):
             nc.vector.quantize_mx(out=words(a, z), scales=scales[:, a:z], in_=grouped[:, J * a : J * z])
@@ -138,7 +136,7 @@ def tile_picked_pair_lin_gate_sub_e_kernel(tc, xT, w, b, offs, out):
             grouped_w1[:, halves[0], :], raw[1, 0][:].rearrange("p j n -> p n j"), 1.0, 0.0, MULT, ADD
         )
         round_w(nc.vector.tensor_copy, grouped_w1[:, halves[1], :], raw[1, 1])
-        codes[1] = keep.tile([P, V], U32, name="codes_hi", tag="raw11", align_bytes=64)
+        codes = keep.tile([P, S], U32, name="codes", tag="raw10", align_bytes=64)
         quantize(V + hi, S)
         quantize_w(1, grouped_w1, slice(0, N), "w_codes1")
         product(1, 0, hi, 0)
@@ -153,7 +151,6 @@ def tile_picked_pair_lin_gate_sub_e_kernel(tc, xT, w, b, offs, out):
         grouped_w0b = keep.tile([P, M, J], BF16, name="grouped_w0b", align_bytes=64)
         round_w(nc.vector.tensor_copy, grouped_w0a[:], raw[0, 0])
         round_w(nc.scalar.copy, grouped_w0b[:], raw[0, 1])
-        codes[0] = keep.tile([P, V], U32, name="codes_lo", tag="raw00", align_bytes=64)
         quantize(hi, V)
         quantize_w(0, grouped_w0a, halves[0], "w_codes0")
         product(0, 0, hi, 6)

@@ -23,6 +23,7 @@ PIECE = 256
 THIRD = S // 3
 LOADS = ((2816, 1280), (2560, 1536), (2304, 1024, 768), (2112, 1056, 544, 256, 128))
 ASSIST = (384, 384, 0, 128)
+CUT = 160
 
 
 def tile_picked_pair_lin_gate_sub_e_kernel(tc, xT, w, b, offs, out):
@@ -36,11 +37,8 @@ def tile_picked_pair_lin_gate_sub_e_kernel(tc, xT, w, b, offs, out):
         list_sb = keep.tile([P, S // 16], U16, name="list_sb")
         planes = [keep.tile([P, T], F32, name=f"plane{j}") for j in range(J)]
         rounded = [keep.tile([P, T], BF16, name=f"rounded{j}") for j in range(J)]
-        raw = {
-            (d, m): keep.tile([P, J, M], F32, name=f"raw{d}{m}", tag=f"raw{d}{m}", align_bytes=64)
-            for d in range(2)
-            for m in range(2)
-        }
+        raw_w1 = [keep.tile([P, J, M], F32, name=f"raw_w1{m}", tag=f"raw_w1{m}", align_bytes=64) for m in range(2)]
+        raw_w0 = keep.tile([P, J, N], F32, name="raw_w0")
         bias = keep.tile([P, 2, 1], F32, name="bias")
 
         def loads(j):
@@ -52,9 +50,10 @@ def tile_picked_pair_lin_gate_sub_e_kernel(tc, xT, w, b, offs, out):
                 nc.sync.dma_start(planes[j][:, cols], x_rows[:, j, cols])
             if j == 0:
                 nc.sync.dma_start(list_sb[:], offs)
-        for d in (1, 0):
-            for m in range(2):
-                nc.sync.dma_start(raw[d, m][:], w[d].rearrange("(p j) n -> p j n", j=J)[:, :, m * M : (m + 1) * M])
+        w_rows = [w[d].rearrange("(p j) n -> p j n", j=J) for d in range(2)]
+        for m in range(2):
+            nc.sync.dma_start(raw_w1[m][:], w_rows[1][:, :, m * M : (m + 1) * M])
+        nc.sync.dma_start(raw_w0[:], w_rows[0])
         with nc.allow_non_contiguous_dma(reason="one bias value a partition for each half of the channels"):
             nc.sync.dma_start(bias[:], b.rearrange("(m p) o -> p m o", p=P))
 
@@ -63,23 +62,20 @@ def tile_picked_pair_lin_gate_sub_e_kernel(tc, xT, w, b, offs, out):
         nc.vector.memset(warm[:], 0.0)
         nc.scalar.activation(warm_out[:], warm[:], SIGMOID)
 
-        w_codes = {}
+        w_codes = [keep.tile([P, N], U32, name=f"w_codes{d}", align_bytes=64) for d in range(2)]
         w_scales = [keep.tile([P, N], U8, name=f"w_scales{d}", align_bytes=64) for d in range(2)]
 
         def round_w(copy, grouped_w, rows):
             copy(
                 grouped_w.rearrange("p (c i) j -> p c j i", i=4),
-                rows[:].rearrange("p j (c i) -> p c j i", i=4),
+                rows.rearrange("p j (c i) -> p c j i", i=4),
             )
 
-        def quantize_w(d, grouped_w, cols, tag):
-            made = keep.tile([P, cols.stop - cols.start], U32, name=f"w_codes{d}_{cols.start}", tag=tag, align_bytes=64)
-            for a in range(cols.start, cols.stop, M):
-                w_codes[d, a // M] = made[:, a - cols.start : a - cols.start + M].bitcast(FP8X4)
+        def quantize_w(d, grouped_w, cols):
             nc.vector.quantize_mx(
-                out=made[:].bitcast(FP8X4),
+                out=w_codes[d][:, cols].bitcast(FP8X4),
                 scales=w_scales[d][:, cols],
-                in_=grouped_w[:].rearrange("p n j -> p (n j)"),
+                in_=grouped_w[:, cols, :].rearrange("p n j -> p (n j)"),
             )
 
         def picks(a, z):
@@ -118,7 +114,7 @@ def tile_picked_pair_lin_gate_sub_e_kernel(tc, xT, w, b, offs, out):
             y[d, m, a] = psum.tile([P, PIECE], F32, name=f"y{d}_{m}_{a}", tag=f"bank{bank}")[:]
             nc.tensor.matmul_mx(
                 out=y[d, m, a],
-                lhsT=w_codes[d, m],
+                lhsT=w_codes[d][:, cols].bitcast(FP8X4),
                 lhsT_scale=w_scales[d][:, cols],
                 rhs=words(first, first + PIECE),
                 rhs_scale=scales[:, first : first + PIECE],
@@ -133,12 +129,12 @@ def tile_picked_pair_lin_gate_sub_e_kernel(tc, xT, w, b, offs, out):
         halves = (slice(0, M), slice(M, N))
         grouped_w1 = keep.tile([P, N, J], BF16, name="grouped_w1", tag="grouped_w", align_bytes=64)
         nc.gpsimd.tensor_scalar(
-            grouped_w1[:, halves[0], :], raw[1, 0][:].rearrange("p j n -> p n j"), 1.0, 0.0, MULT, ADD
+            grouped_w1[:, halves[0], :], raw_w1[0][:].rearrange("p j n -> p n j"), 1.0, 0.0, MULT, ADD
         )
-        round_w(nc.vector.tensor_copy, grouped_w1[:, halves[1], :], raw[1, 1])
-        codes = keep.tile([P, S], U32, name="codes", tag="raw10", align_bytes=64)
+        round_w(nc.vector.tensor_copy, grouped_w1[:, halves[1], :], raw_w1[1][:])
+        codes = keep.tile([P, S], U32, name="codes", tag="raw_w10", align_bytes=64)
         quantize(V + hi, S)
-        quantize_w(1, grouped_w1, slice(0, N), "w_codes1")
+        quantize_w(1, grouped_w1, slice(0, N))
         product(1, 0, hi, 0)
         product(1, 1, hi, 3)
         quantize(V + mid, V + hi)
@@ -147,12 +143,11 @@ def tile_picked_pair_lin_gate_sub_e_kernel(tc, xT, w, b, offs, out):
         quantize(V + lo, V + mid)
         product(1, 0, lo, 2)
         product(1, 1, lo, 5)
-        grouped_w0a = keep.tile([P, M, J], BF16, name="grouped_w0a", tag="grouped_w", align_bytes=64)
-        grouped_w0b = keep.tile([P, M, J], BF16, name="grouped_w0b", align_bytes=64)
-        round_w(nc.vector.tensor_copy, grouped_w0a[:], raw[0, 0])
-        round_w(nc.scalar.copy, grouped_w0b[:], raw[0, 1])
+        grouped_w0 = keep.tile([P, N, J], BF16, name="grouped_w0", tag="grouped_w", align_bytes=64)
+        round_w(nc.vector.tensor_copy, grouped_w0[:, :CUT, :], raw_w0[:, :, :CUT])
+        round_w(nc.scalar.copy, grouped_w0[:, CUT:, :], raw_w0[:, :, CUT:])
         quantize(hi, V)
-        quantize_w(0, grouped_w0a, halves[0], "w_codes0")
+        quantize_w(0, grouped_w0, halves[0])
         product(0, 0, hi, 6)
         for m in range(2):
             for a in (hi, mid, lo):
@@ -161,7 +156,7 @@ def tile_picked_pair_lin_gate_sub_e_kernel(tc, xT, w, b, offs, out):
         product(0, 0, mid, 7)
         quantize(lo, mid)
         product(0, 0, lo, 0)
-        quantize_w(0, grouped_w0b, halves[1], "grouped_w")
+        quantize_w(0, grouped_w0, halves[1])
         for i, a in enumerate((hi, mid, lo)):
             product(0, 1, a, (1, 2, 3)[i])
 

@@ -21,8 +21,8 @@ J = 4
 M = 128
 PIECE = 256
 THIRD = S // 3
-LOADS = ((2816, 1280), (2560, 1536), (2304, 1024, 768), (2112, 1056, 544, 256, 128))
-ASSIST = (384, 384, 0, 128)
+LOADS = ((T,), (T,), (2816, 1280), (2112, 1056, 544, 256, 128))
+ON_VECTOR = (None, None, (1536, 832), (2112, 1056, 544, 256, 0))
 CUT = 160
 
 
@@ -36,7 +36,6 @@ def tile_picked_pair_lin_gate_sub_e_kernel(tc, xT, w, b, offs, out):
 
         list_sb = keep.tile([P, S // 16], U16, name="list_sb")
         planes = [keep.tile([P, T], F32, name=f"plane{j}") for j in range(J)]
-        rounded = [keep.tile([P, T], BF16, name=f"rounded{j}") for j in range(J)]
         raw_w1 = [keep.tile([P, J, M], F32, name=f"raw_w1{m}", tag=f"raw_w1{m}", align_bytes=64) for m in range(2)]
         raw_w0 = keep.tile([P, J, N], F32, name="raw_w0")
         bias = keep.tile([P, 2, 1], F32, name="bias")
@@ -84,18 +83,26 @@ def tile_picked_pair_lin_gate_sub_e_kernel(tc, xT, w, b, offs, out):
         grouped = keep.tile([P, S * J], BF16, name="grouped", align_bytes=64)
         by_entry = grouped[:].rearrange("p (n j) -> p n j", j=J)
 
-        for j in range(J):
-            vector_stop = T - ASSIST[j]
-            for cols in loads(j):
-                z = min(cols.stop, vector_stop)
-                if cols.start < z:
-                    nc.vector.tensor_copy(rounded[j][:, cols.start : z], planes[j][:, cols.start : z])
-            if vector_stop < T:
-                nc.scalar.copy(rounded[j][:, vector_stop:], planes[j][:, vector_stop:])
+        for j in range(2):
+            nc.vector.tensor_copy(by_entry[:, 2 * THIRD : S, j], planes[j][:].indirect(picks(2 * THIRD, S)))
+            for i in range(2):
+                a, z = i * THIRD, (i + 1) * THIRD
+                picked = keep.tile([P, THIRD], BF16, name=f"picked{j}_{i}", tag=f"picked{i}")
+                nc.scalar.activation(picked[:], planes[j][:].indirect(picks(a, z)), COPY)
+                nc.vector.tensor_copy(by_entry[:, a:z, j], picked[:])
+
+        for j in range(2, J):
+            rounded = keep.tile([P, T], BF16, name=f"rounded{j}")
+            for cols, n in zip(loads(j), ON_VECTOR[j]):
+                cut = cols.start + n
+                if n:
+                    nc.vector.tensor_copy(rounded[:, cols.start : cut], planes[j][:, cols.start : cut])
+                if cut < cols.stop:
+                    nc.scalar.copy(rounded[:, cut : cols.stop], planes[j][:, cut : cols.stop])
             nc.vector.tensor_copy(by_entry[:, 2 * THIRD : S, j], planes[j][:].indirect(picks(2 * THIRD, S)))
             shares = ((0, 2 * THIRD),) if j < J - 1 else ((THIRD, 2 * THIRD), (0, THIRD))
             for a, z in shares:
-                nc.scalar.activation(by_entry[:, a:z, j], rounded[j][:].indirect(picks(a, z)), COPY)
+                nc.scalar.activation(by_entry[:, a:z, j], rounded[:].indirect(picks(a, z)), COPY)
 
         scales = keep.tile([P, S], U8, name="scales", align_bytes=64)
         gate = [keep.tile([P, V], F32, name=f"gate{m}") for m in range(2)]

@@ -21,8 +21,8 @@ J = 4
 M = 128
 PIECE = 256
 THIRD = S // 3
-LOADS = ((T,), (T,), (2816, 1280), (2112, 1056, 544, 256, 128))
-ON_VECTOR = (None, None, (1536, 832), (2112, 1056, 544, 256, 0))
+LOADS = ((T,), (T,), (2816, 1280), (2176, 1088, 576, 256))
+ON_VECTOR = (None, None, (1536, 832), (2176, 1088, 384, 128))
 CUT = 160
 
 
@@ -106,7 +106,8 @@ def tile_picked_pair_lin_gate_sub_e_kernel(tc, xT, w, b, offs, out):
 
         scales = keep.tile([P, S], U8, name="scales", align_bytes=64)
         gate = [keep.tile([P, V], F32, name=f"gate{m}") for m in range(2)]
-        result = [keep.tile([P, V], F32, name=f"result{m}") for m in range(2)]
+        result = keep.tile([P, 2, V], F32, name="result")
+        out_rows = out.rearrange("(m p) v -> p m v", p=P)
         y = {}
 
         def words(a, z):
@@ -156,19 +157,21 @@ def tile_picked_pair_lin_gate_sub_e_kernel(tc, xT, w, b, offs, out):
         quantize(hi, V)
         quantize_w(0, grouped_w0, halves[0])
         product(0, 0, hi, 6)
-        for m in range(2):
-            for a in (hi, mid, lo):
-                sigmoid(m, a)
+        order = ((0, hi), (0, mid), (0, lo), (1, lo), (1, mid), (1, hi))
+        for m, a in order:
+            sigmoid(m, a)
         quantize(mid, hi)
         product(0, 0, mid, 7)
         quantize(lo, mid)
         product(0, 0, lo, 0)
         quantize_w(0, grouped_w0, halves[1])
-        for i, a in enumerate((hi, mid, lo)):
-            product(0, 1, a, (1, 2, 3)[i])
+        for i, a in enumerate((lo, mid, hi)):
+            product(0, 1, a, (1, 2, 5)[i])
 
-        for m in range(2):
-            for a in (hi, mid, lo):
-                cols = slice(a, a + PIECE)
-                nc.vector.tensor_tensor(result[m][:, cols], y[0, m, a], gate[m][:, cols], MULT)
-                nc.sync.dma_start(out[m * M : (m + 1) * M, cols], result[m][:, cols])
+        stores = ((slice(0, 1), slice(mid, V)), (slice(0, 2), slice(lo, mid)), (slice(1, 2), slice(mid, V)))
+        for i, (m, a) in enumerate(order):
+            cols = slice(a, a + PIECE)
+            nc.vector.tensor_tensor(result[:, m, cols], y[0, m, a], gate[m][:, cols], MULT)
+            if i % 2:
+                rows, span = stores[i // 2]
+                nc.sync.dma_start(out_rows[:, rows, span], result[:, rows, span])

@@ -21,8 +21,8 @@ J = 4
 M = 128
 PIECE = 256
 THIRD = S // 3
-LOADS = ((T,), (T,), (2816, 1280), (2176, 1088, 576, 256))
-ON_VECTOR = (None, None, (1536, 832), (2176, 1088, 384, 128))
+LOADS = ((T,), (T,), (T,), (2560, 1152, 384))
+ON_VECTOR = (1536, 768, 256)
 CUT = 160
 
 
@@ -91,18 +91,25 @@ def tile_picked_pair_lin_gate_sub_e_kernel(tc, xT, w, b, offs, out):
                 nc.scalar.activation(picked[:], planes[j][:].indirect(picks(a, z)), COPY)
                 nc.vector.tensor_copy(by_entry[:, a:z, j], picked[:])
 
-        for j in range(2, J):
-            rounded = keep.tile([P, T], BF16, name=f"rounded{j}")
-            for cols, n in zip(loads(j), ON_VECTOR[j]):
-                cut = cols.start + n
-                if n:
-                    nc.vector.tensor_copy(rounded[:, cols.start : cut], planes[j][:, cols.start : cut])
-                if cut < cols.stop:
-                    nc.scalar.copy(rounded[:, cut : cols.stop], planes[j][:, cut : cols.stop])
-            nc.vector.tensor_copy(by_entry[:, 2 * THIRD : S, j], planes[j][:].indirect(picks(2 * THIRD, S)))
-            shares = ((0, 2 * THIRD),) if j < J - 1 else ((THIRD, 2 * THIRD), (0, THIRD))
-            for a, z in shares:
-                nc.scalar.activation(by_entry[:, a:z, j], rounded[:].indirect(picks(a, z)), COPY)
+        j = 2
+        nc.vector.tensor_copy(by_entry[:, V:S, j], planes[j][:].indirect(picks(V, S)))
+        for a, z, tag in ((0, 192, "picked0"), (192, THIRD, "rounded"), (THIRD, V, "picked1")):
+            picked = keep.tile([P, z - a], BF16, name=f"picked{j}_{a}", tag=tag)
+            nc.scalar.activation(picked[:], planes[j][:].indirect(picks(a, z)), COPY)
+            if z < V:
+                nc.gpsimd.tensor_scalar(by_entry[:, a:z, j], picked[:], 1.0, 0.0, MULT, ADD)
+            else:
+                nc.vector.tensor_copy(by_entry[:, a:z, j], picked[:])
+
+        j = J - 1
+        rounded = keep.tile([P, T], BF16, name="rounded", tag="rounded")
+        for cols, n in zip(loads(j), ON_VECTOR):
+            cut = cols.start + n
+            nc.vector.tensor_copy(rounded[:, cols.start : cut], planes[j][:, cols.start : cut])
+            nc.scalar.copy(rounded[:, cut : cols.stop], planes[j][:, cut : cols.stop])
+        nc.vector.tensor_copy(by_entry[:, 2 * THIRD : S, j], planes[j][:].indirect(picks(2 * THIRD, S)))
+        for a, z in ((THIRD, 2 * THIRD), (0, THIRD)):
+            nc.scalar.activation(by_entry[:, a:z, j], rounded[:].indirect(picks(a, z)), COPY)
 
         scales = keep.tile([P, S], U8, name="scales", align_bytes=64)
         gate = [keep.tile([P, V], F32, name=f"gate{m}") for m in range(2)]
@@ -168,10 +175,9 @@ def tile_picked_pair_lin_gate_sub_e_kernel(tc, xT, w, b, offs, out):
         for i, a in enumerate((lo, mid, hi)):
             product(0, 1, a, (1, 2, 5)[i])
 
-        stores = ((slice(0, 1), slice(mid, V)), (slice(0, 2), slice(lo, mid)), (slice(1, 2), slice(mid, V)))
-        for i, (m, a) in enumerate(order):
+        for m, a in order:
             cols = slice(a, a + PIECE)
             nc.vector.tensor_tensor(result[:, m, cols], y[0, m, a], gate[m][:, cols], MULT)
-            if i % 2:
-                rows, span = stores[i // 2]
-                nc.sync.dma_start(out_rows[:, rows, span], result[:, rows, span])
+            if (m, a) != (1, mid):
+                span = slice(mid, V) if (m, a) == (1, hi) else cols
+                nc.sync.dma_start(out_rows[:, m, span], result[:, m, span])

@@ -21,8 +21,8 @@ J = 4
 M = 128
 PIECE = 256
 THIRD = S // 3
-LOADS = ((T,), (T,), (T,), (2560, 1152, 384))
-ON_VECTOR = (1536, 768, 256)
+LOADS = ((T,), (T,), (T,), (2880, 960, 256))
+ON_VECTOR = (1920, 640, 160)
 CUT = 160
 
 
@@ -99,7 +99,7 @@ def tile_picked_pair_lin_gate_sub_e_kernel(tc, xT, w, b, offs, out):
             if z < V:
                 nc.gpsimd.tensor_scalar(by_entry[:, a:z, j], picked[:], 1.0, 0.0, MULT, ADD)
             else:
-                nc.vector.tensor_copy(by_entry[:, a:z, j], picked[:])
+                nc.scalar.copy(by_entry[:, a:z, j], picked[:])
 
         j = J - 1
         rounded = keep.tile([P, T], BF16, name="rounded", tag="rounded")

@@ -92,11 +92,11 @@ def tile_picked_pair_lin_gate_sub_e_kernel(tc, xT, w, b, offs, out):
                 nc.vector.tensor_copy(by_entry[:, a:z, j], picked[:])
 
         j = 2
-        nc.vector.tensor_copy(by_entry[:, V:S, j], planes[j][:].indirect(picks(V, S)))
-        for a, z, tag in ((0, 192, "picked0"), (192, THIRD, "rounded"), (THIRD, V, "picked1")):
+        nc.vector.tensor_copy(by_entry[:, 704:S, j], planes[j][:].indirect(picks(704, S)))
+        for a, z, tag in ((0, 192, "picked0"), (192, 448, "rounded"), (448, 704, "picked1")):
             picked = keep.tile([P, z - a], BF16, name=f"picked{j}_{a}", tag=tag)
             nc.scalar.activation(picked[:], planes[j][:].indirect(picks(a, z)), COPY)
-            if z < V:
+            if z < 704:
                 nc.gpsimd.tensor_scalar(by_entry[:, a:z, j], picked[:], 1.0, 0.0, MULT, ADD)
             else:
                 nc.scalar.copy(by_entry[:, a:z, j], picked[:])

@@ -148,8 +148,9 @@ def tile_picked_pair_lin_gate_sub_e_kernel(tc, xT, w, b, offs, out):
         )
         round_w(nc.vector.tensor_copy, grouped_w1[:, halves[1], :], raw_w1[1][:])
         codes = keep.tile([P, S], U32, name="codes", tag="raw_w10", align_bytes=64)
+        quantize_w(1, grouped_w1, halves[0])
         quantize(V + hi, S)
-        quantize_w(1, grouped_w1, slice(0, N))
+        quantize_w(1, grouped_w1, halves[1])
         product(1, 0, hi, 0)
         product(1, 1, hi, 3)
         quantize(V + mid, V + hi)

@@ -22,7 +22,7 @@ M = 128
 PIECE = 256
 THIRD = S // 3
 LOADS = ((T,), (T,), (T,), (2880, 960, 256))
-ON_VECTOR = (1920, 640, 160)
+ON_VECTOR = (1920, 640, 96)
 CUT = 160
 
 
@@ -105,7 +105,8 @@ def tile_picked_pair_lin_gate_sub_e_kernel(tc, xT, w, b, offs, out):
         rounded = keep.tile([P, T], BF16, name="rounded", tag="rounded")
         for cols, n in zip(loads(j), ON_VECTOR):
             cut = cols.start + n
-            nc.vector.tensor_copy(rounded[:, cols.start : cut], planes[j][:, cols.start : cut])
+            other = nc.gpsimd if cols.stop == T else nc.vector
+            other.tensor_copy(rounded[:, cols.start : cut], planes[j][:, cols.start : cut])
             nc.scalar.copy(rounded[:, cut : cols.stop], planes[j][:, cut : cols.stop])
         nc.vector.tensor_copy(by_entry[:, 2 * THIRD : S, j], planes[j][:].indirect(picks(2 * THIRD, S)))
         for a, z in ((THIRD, 2 * THIRD), (0, THIRD)):

@@ -23,7 +23,7 @@ PIECE = 256
 THIRD = S // 3
 LOADS = ((T,), (T,), (T,), (2880, 960, 256))
 ON_VECTOR = (1920, 640, 96)
-CUT = 160
+CUT = 192
 
 
 def tile_picked_pair_lin_gate_sub_e_kernel(tc, xT, w, b, offs, out):

@@ -23,7 +23,6 @@ PIECE = 256
 THIRD = S // 3
 LOADS = ((T,), (T,), (T,), (2880, 960, 256))
 ON_VECTOR = (1920, 640, 96)
-CUT = 192
 
 
 def tile_picked_pair_lin_gate_sub_e_kernel(tc, xT, w, b, offs, out):
@@ -161,25 +160,25 @@ def tile_picked_pair_lin_gate_sub_e_kernel(tc, xT, w, b, offs, out):
         product(1, 0, lo, 2)
         product(1, 1, lo, 5)
         grouped_w0 = keep.tile([P, N, J], BF16, name="grouped_w0", tag="grouped_w", align_bytes=64)
-        round_w(nc.vector.tensor_copy, grouped_w0[:, :CUT, :], raw_w0[:, :, :CUT])
-        round_w(nc.scalar.copy, grouped_w0[:, CUT:, :], raw_w0[:, :, CUT:])
+        round_w(nc.vector.tensor_copy, grouped_w0[:], raw_w0[:])
         quantize(hi, V)
         quantize_w(0, grouped_w0, halves[0])
         product(0, 0, hi, 6)
-        order = ((0, hi), (0, mid), (0, lo), (1, lo), (1, mid), (1, hi))
+        quantize_w(0, grouped_w0, halves[1])
+        product(0, 1, hi, 7)
+        order = ((0, hi), (1, hi), (0, mid), (0, lo), (1, mid), (1, lo))
         for m, a in order:
             sigmoid(m, a)
         quantize(mid, hi)
-        product(0, 0, mid, 7)
+        product(0, 0, mid, 0)
+        product(0, 1, mid, 3)
         quantize(lo, mid)
-        product(0, 0, lo, 0)
-        quantize_w(0, grouped_w0, halves[1])
-        for i, a in enumerate((lo, mid, hi)):
-            product(0, 1, a, (1, 2, 5)[i])
+        product(0, 0, lo, 1)
+        product(0, 1, lo, 2)
 
         for m, a in order:
             cols = slice(a, a + PIECE)
             nc.vector.tensor_tensor(result[:, m, cols], y[0, m, a], gate[m][:, cols], MULT)
             if (m, a) != (1, mid):
-                span = slice(mid, V) if (m, a) == (1, hi) else cols
+                span = slice(lo, hi) if (m, a) == (1, lo) else cols
                 nc.sync.dma_start(out_rows[:, m, span], result[:, m, span])

@@ -51,7 +51,8 @@ def tile_picked_pair_lin_gate_sub_e_kernel(tc, xT, w, b, offs, out):
         w_rows = [w[d].rearrange("(p j) n -> p j n", j=J) for d in range(2)]
         for m in range(2):
             nc.sync.dma_start(raw_w1[m][:], w_rows[1][:, :, m * M : (m + 1) * M])
-        nc.sync.dma_start(raw_w0[:], w_rows[0])
+        for rows in (slice(0, 2), slice(2, J)):
+            nc.sync.dma_start(raw_w0[:, rows, :], w_rows[0][:, rows, :])
         with nc.allow_non_contiguous_dma(reason="one bias value a partition for each half of the channels"):
             nc.sync.dma_start(bias[:], b.rearrange("(m p) o -> p m o", p=P))
 
@@ -179,6 +180,6 @@ def tile_picked_pair_lin_gate_sub_e_kernel(tc, xT, w, b, offs, out):
         for m, a in order:
             cols = slice(a, a + PIECE)
             nc.vector.tensor_tensor(result[:, m, cols], y[0, m, a], gate[m][:, cols], MULT)
-            if (m, a) != (1, mid):
-                span = slice(lo, hi) if (m, a) == (1, lo) else cols
+            if a != mid:
+                span = slice(lo, hi) if a == lo else cols
                 nc.sync.dma_start(out_rows[:, m, span], result[:, m, span])

@@ -21,13 +21,14 @@ J = 4
 M = 128
 PIECE = 256
 THIRD = S // 3
-LOADS = ((T,), (T,), (T,), (2880, 960, 256))
-ON_VECTOR = (1920, 640, 96)
+LOAD_ORDER = (2, 0, 1, 3)
 
 
 def tile_picked_pair_lin_gate_sub_e_kernel(tc, xT, w, b, offs, out):
     nc = tc.nc
     x_rows = xT.rearrange("(p j) t -> p j t", j=J)
+    w_rows = [w[d].rearrange("(p j) n -> p j n", j=J) for d in range(2)]
+    halves = (slice(0, M), slice(M, N))
 
     with ExitStack() as ctx:
         keep = ctx.enter_context(tc.tile_pool(name="keep", bufs=1))
@@ -35,24 +36,20 @@ def tile_picked_pair_lin_gate_sub_e_kernel(tc, xT, w, b, offs, out):
 
         list_sb = keep.tile([P, S // 16], U16, name="list_sb")
         planes = [keep.tile([P, T], F32, name=f"plane{j}") for j in range(J)]
-        raw_w1 = [keep.tile([P, J, M], F32, name=f"raw_w1{m}", tag=f"raw_w1{m}", align_bytes=64) for m in range(2)]
-        raw_w0 = keep.tile([P, J, N], F32, name="raw_w0")
+        raw_w = {
+            (d, m): keep.tile([P, J, M], F32, name=f"raw_w{d}{m}", tag=f"raw_w{d}{m}", align_bytes=64)
+            for d in range(2)
+            for m in range(2)
+        }
         bias = keep.tile([P, 2, 1], F32, name="bias")
 
-        def loads(j):
-            edges = [sum(LOADS[j][:i]) for i in range(len(LOADS[j]) + 1)]
-            return [slice(a, z) for a, z in zip(edges, edges[1:])]
-
-        for j in range(J):
-            for cols in loads(j):
-                nc.sync.dma_start(planes[j][:, cols], x_rows[:, j, cols])
-            if j == 0:
+        for j in LOAD_ORDER:
+            nc.sync.dma_start(planes[j][:], x_rows[:, j, :])
+            if j == LOAD_ORDER[0]:
                 nc.sync.dma_start(list_sb[:], offs)
-        w_rows = [w[d].rearrange("(p j) n -> p j n", j=J) for d in range(2)]
-        for m in range(2):
-            nc.sync.dma_start(raw_w1[m][:], w_rows[1][:, :, m * M : (m + 1) * M])
-        for rows in (slice(0, 2), slice(2, J)):
-            nc.sync.dma_start(raw_w0[:, rows, :], w_rows[0][:, rows, :])
+        for d in (1, 0):
+            for m in range(2):
+                nc.sync.dma_start(raw_w[d, m][:], w_rows[d][:, :, halves[m]])
         with nc.allow_non_contiguous_dma(reason="one bias value a partition for each half of the channels"):
             nc.sync.dma_start(bias[:], b.rearrange("(m p) o -> p m o", p=P))
 
@@ -61,56 +58,38 @@ def tile_picked_pair_lin_gate_sub_e_kernel(tc, xT, w, b, offs, out):
         nc.vector.memset(warm[:], 0.0)
         nc.scalar.activation(warm_out[:], warm[:], SIGMOID)
 
-        w_codes = [keep.tile([P, N], U32, name=f"w_codes{d}", align_bytes=64) for d in range(2)]
-        w_scales = [keep.tile([P, N], U8, name=f"w_scales{d}", align_bytes=64) for d in range(2)]
-
-        def round_w(copy, grouped_w, rows):
-            copy(
-                grouped_w.rearrange("p (c i) j -> p c j i", i=4),
-                rows.rearrange("p j (c i) -> p c j i", i=4),
-            )
-
-        def quantize_w(d, grouped_w, cols):
-            nc.vector.quantize_mx(
-                out=w_codes[d][:, cols].bitcast(FP8X4),
-                scales=w_scales[d][:, cols],
-                in_=grouped_w[:, cols, :].rearrange("p n j -> p (n j)"),
-            )
-
-        def picks(a, z):
-            return list_sb[:, a // 16 : z // 16]
-
         grouped = keep.tile([P, S * J], BF16, name="grouped", align_bytes=64)
         by_entry = grouped[:].rearrange("p (n j) -> p n j", j=J)
 
-        for j in range(2):
-            nc.vector.tensor_copy(by_entry[:, 2 * THIRD : S, j], planes[j][:].indirect(picks(2 * THIRD, S)))
-            for i in range(2):
-                a, z = i * THIRD, (i + 1) * THIRD
-                picked = keep.tile([P, THIRD], BF16, name=f"picked{j}_{i}", tag=f"picked{i}")
-                nc.scalar.activation(picked[:], planes[j][:].indirect(picks(a, z)), COPY)
-                nc.vector.tensor_copy(by_entry[:, a:z, j], picked[:])
+        def picked(j, a, z):
+            return planes[j][:].indirect(list_sb[:, a // 16 : z // 16])
 
-        j = 2
-        nc.vector.tensor_copy(by_entry[:, 704:S, j], planes[j][:].indirect(picks(704, S)))
-        for a, z, tag in ((0, 192, "picked0"), (192, 448, "rounded"), (448, 704, "picked1")):
-            picked = keep.tile([P, z - a], BF16, name=f"picked{j}_{a}", tag=tag)
-            nc.scalar.activation(picked[:], planes[j][:].indirect(picks(a, z)), COPY)
-            if z < 704:
-                nc.gpsimd.tensor_scalar(by_entry[:, a:z, j], picked[:], 1.0, 0.0, MULT, ADD)
-            else:
-                nc.scalar.copy(by_entry[:, a:z, j], picked[:])
-
+        for j in LOAD_ORDER[:-1]:
+            cut = 2 * THIRD if j == 2 else V
+            nc.vector.tensor_copy(by_entry[:, cut:S, j], picked(j, cut, S))
+            nc.scalar.activation(by_entry[:, 0:cut, j], picked(j, 0, cut), COPY)
         j = J - 1
-        rounded = keep.tile([P, T], BF16, name="rounded", tag="rounded")
-        for cols, n in zip(loads(j), ON_VECTOR):
-            cut = cols.start + n
-            other = nc.gpsimd if cols.stop == T else nc.vector
-            other.tensor_copy(rounded[:, cols.start : cut], planes[j][:, cols.start : cut])
-            nc.scalar.copy(rounded[:, cut : cols.stop], planes[j][:, cut : cols.stop])
-        nc.vector.tensor_copy(by_entry[:, 2 * THIRD : S, j], planes[j][:].indirect(picks(2 * THIRD, S)))
+        nc.vector.tensor_copy(by_entry[:, 2 * THIRD : S, j], picked(j, 2 * THIRD, S))
         for a, z in ((THIRD, 2 * THIRD), (0, THIRD)):
-            nc.scalar.activation(by_entry[:, a:z, j], rounded[:].indirect(picks(a, z)), COPY)
+            nc.scalar.activation(by_entry[:, a:z, j], picked(j, a, z), COPY)
+
+        w_codes = [keep.tile([P, N], U32, name=f"w_codes{d}", align_bytes=64) for d in range(2)]
+        w_scales = [keep.tile([P, N], U8, name=f"w_scales{d}", align_bytes=64) for d in range(2)]
+        grouped_w = {}
+
+        def round_w(d, m, copy):
+            grouped_w[d, m] = keep.tile([P, M, J], BF16, name=f"grouped_w{d}{m}", tag=f"grouped_w{m}", align_bytes=64)
+            copy(
+                grouped_w[d, m][:].rearrange("p (c i) j -> p c j i", i=4),
+                raw_w[d, m][:].rearrange("p j (c i) -> p c j i", i=4),
+            )
+
+        def quantize_w(d, m):
+            nc.vector.quantize_mx(
+                out=w_codes[d][:, halves[m]].bitcast(FP8X4),
+                scales=w_scales[d][:, halves[m]],
+                in_=grouped_w[d, m][:].rearrange("p n j -> p (n j)"),
+            )
 
         scales = keep.tile([P, S], U8, name="scales", align_bytes=64)
         gate = [keep.tile([P, V], F32, name=f"gate{m}") for m in range(2)]
@@ -121,17 +100,21 @@ def tile_picked_pair_lin_gate_sub_e_kernel(tc, xT, w, b, offs, out):
         def words(a, z):
             return codes[:, a:z].bitcast(FP8X4)
 
-        def quantize(a, z):
-            nc.vector.quantize_mx(out=words(a, z), scales=scales[:, a:z], in_=grouped[:, J * a : J * z])
+        def quantize(d, a):
+            first = d * V + a
+            nc.vector.quantize_mx(
+                out=words(first, first + PIECE),
+                scales=scales[:, first : first + PIECE],
+                in_=grouped[:, J * first : J * (first + PIECE)],
+            )
 
         def product(d, m, a, bank):
             first = d * V + a
-            cols = slice(m * M, (m + 1) * M)
             y[d, m, a] = psum.tile([P, PIECE], F32, name=f"y{d}_{m}_{a}", tag=f"bank{bank}")[:]
             nc.tensor.matmul_mx(
                 out=y[d, m, a],
-                lhsT=w_codes[d][:, cols].bitcast(FP8X4),
-                lhsT_scale=w_scales[d][:, cols],
+                lhsT=w_codes[d][:, halves[m]].bitcast(FP8X4),
+                lhsT_scale=w_scales[d][:, halves[m]],
                 rhs=words(first, first + PIECE),
                 rhs_scale=scales[:, first : first + PIECE],
                 start=True,
@@ -142,44 +125,39 @@ def tile_picked_pair_lin_gate_sub_e_kernel(tc, xT, w, b, offs, out):
             nc.scalar.activation(gate[m][:, a : a + PIECE], y[1, m, a], SIGMOID, bias=bias[:, m, :])
 
         hi, mid, lo = 2 * PIECE, PIECE, 0
-        halves = (slice(0, M), slice(M, N))
-        grouped_w1 = keep.tile([P, N, J], BF16, name="grouped_w1", tag="grouped_w", align_bytes=64)
-        nc.gpsimd.tensor_scalar(
-            grouped_w1[:, halves[0], :], raw_w1[0][:].rearrange("p j n -> p n j"), 1.0, 0.0, MULT, ADD
-        )
-        round_w(nc.vector.tensor_copy, grouped_w1[:, halves[1], :], raw_w1[1][:])
+        grouped_w[1, 0] = keep.tile([P, M, J], BF16, name="grouped_w10", tag="grouped_w0", align_bytes=64)
+        nc.gpsimd.tensor_scalar(grouped_w[1, 0][:], raw_w[1, 0][:].rearrange("p j n -> p n j"), 1.0, 0.0, MULT, ADD)
+        round_w(1, 1, nc.vector.tensor_copy)
         codes = keep.tile([P, S], U32, name="codes", tag="raw_w10", align_bytes=64)
-        quantize_w(1, grouped_w1, halves[0])
-        quantize(V + hi, S)
-        quantize_w(1, grouped_w1, halves[1])
+        quantize_w(1, 0)
+        quantize(1, hi)
+        quantize_w(1, 1)
         product(1, 0, hi, 0)
-        product(1, 1, hi, 3)
-        quantize(V + mid, V + hi)
+        product(1, 1, hi, 2)
+        quantize(1, mid)
         product(1, 0, mid, 1)
-        product(1, 1, mid, 4)
-        quantize(V + lo, V + mid)
-        product(1, 0, lo, 2)
+        product(1, 1, mid, 3)
+        quantize(1, lo)
+        product(1, 0, lo, 4)
         product(1, 1, lo, 5)
-        grouped_w0 = keep.tile([P, N, J], BF16, name="grouped_w0", tag="grouped_w", align_bytes=64)
-        round_w(nc.vector.tensor_copy, grouped_w0[:], raw_w0[:])
-        quantize(hi, V)
-        quantize_w(0, grouped_w0, halves[0])
-        product(0, 0, hi, 6)
-        quantize_w(0, grouped_w0, halves[1])
-        product(0, 1, hi, 7)
-        order = ((0, hi), (1, hi), (0, mid), (0, lo), (1, mid), (1, lo))
+        round_w(0, 0, nc.vector.tensor_copy)
+        round_w(0, 1, nc.scalar.copy)
+        order = ((0, hi), (0, mid), (1, hi), (1, mid), (0, lo), (1, lo))
         for m, a in order:
             sigmoid(m, a)
-        quantize(mid, hi)
-        product(0, 0, mid, 0)
-        product(0, 1, mid, 3)
-        quantize(lo, mid)
-        product(0, 0, lo, 1)
-        product(0, 1, lo, 2)
+        quantize(0, hi)
+        quantize_w(0, 0)
+        product(0, 0, hi, 6)
+        quantize(0, mid)
+        product(0, 0, mid, 7)
+        quantize_w(0, 1)
+        product(0, 1, hi, 0)
+        product(0, 1, mid, 1)
+        quantize(0, lo)
+        product(0, 0, lo, 2)
+        product(0, 1, lo, 3)
 
         for m, a in order:
             cols = slice(a, a + PIECE)
             nc.vector.tensor_tensor(result[:, m, cols], y[0, m, a], gate[m][:, cols], MULT)
-            if a != mid:
-                span = slice(lo, hi) if a == lo else cols
-                nc.sync.dma_start(out_rows[:, m, span], result[:, m, span])
+            nc.sync.dma_start(out_rows[:, m, cols], result[:, m, cols])

@@ -22,6 +22,7 @@ M = 128
 PIECE = 256
 THIRD = S // 3
 LOAD_ORDER = (2, 0, 1, 3)
+W0_ON_VECTOR = 192
 
 
 def tile_picked_pair_lin_gate_sub_e_kernel(tc, xT, w, b, offs, out):
@@ -36,20 +37,18 @@ def tile_picked_pair_lin_gate_sub_e_kernel(tc, xT, w, b, offs, out):
 
         list_sb = keep.tile([P, S // 16], U16, name="list_sb")
         planes = [keep.tile([P, T], F32, name=f"plane{j}") for j in range(J)]
-        raw_w = {
-            (d, m): keep.tile([P, J, M], F32, name=f"raw_w{d}{m}", tag=f"raw_w{d}{m}", align_bytes=64)
-            for d in range(2)
-            for m in range(2)
-        }
+        raw_w1 = [keep.tile([P, J, M], F32, name=f"raw_w1{m}", tag=f"raw_w1{m}", align_bytes=64) for m in range(2)]
+        raw_w0 = keep.tile([P, J, N], F32, name="raw_w0")
         bias = keep.tile([P, 2, 1], F32, name="bias")
 
         for j in LOAD_ORDER:
             nc.sync.dma_start(planes[j][:], x_rows[:, j, :])
             if j == LOAD_ORDER[0]:
                 nc.sync.dma_start(list_sb[:], offs)
-        for d in (1, 0):
-            for m in range(2):
-                nc.sync.dma_start(raw_w[d, m][:], w_rows[d][:, :, halves[m]])
+        for m in range(2):
+            nc.sync.dma_start(raw_w1[m][:], w_rows[1][:, :, halves[m]])
+        for rows in (slice(0, 2), slice(2, J)):
+            nc.sync.dma_start(raw_w0[:, rows, :], w_rows[0][:, rows, :])
         with nc.allow_non_contiguous_dma(reason="one bias value a partition for each half of the channels"):
             nc.sync.dma_start(bias[:], b.rearrange("(m p) o -> p m o", p=P))
 
@@ -77,18 +76,17 @@ def tile_picked_pair_lin_gate_sub_e_kernel(tc, xT, w, b, offs, out):
         w_scales = [keep.tile([P, N], U8, name=f"w_scales{d}", align_bytes=64) for d in range(2)]
         grouped_w = {}
 
-        def round_w(d, m, copy):
-            grouped_w[d, m] = keep.tile([P, M, J], BF16, name=f"grouped_w{d}{m}", tag=f"grouped_w{m}", align_bytes=64)
+        def round_w(copy, grouped_cols, rows):
             copy(
-                grouped_w[d, m][:].rearrange("p (c i) j -> p c j i", i=4),
-                raw_w[d, m][:].rearrange("p j (c i) -> p c j i", i=4),
+                grouped_cols.rearrange("p (c i) j -> p c j i", i=4),
+                rows.rearrange("p j (c i) -> p c j i", i=4),
             )
 
         def quantize_w(d, m):
             nc.vector.quantize_mx(
                 out=w_codes[d][:, halves[m]].bitcast(FP8X4),
                 scales=w_scales[d][:, halves[m]],
-                in_=grouped_w[d, m][:].rearrange("p n j -> p (n j)"),
+                in_=grouped_w[d][:, halves[m], :].rearrange("p n j -> p (n j)"),
             )
 
         scales = keep.tile([P, S], U8, name="scales", align_bytes=64)
@@ -125,9 +123,11 @@ def tile_picked_pair_lin_gate_sub_e_kernel(tc, xT, w, b, offs, out):
             nc.scalar.activation(gate[m][:, a : a + PIECE], y[1, m, a], SIGMOID, bias=bias[:, m, :])
 
         hi, mid, lo = 2 * PIECE, PIECE, 0
-        grouped_w[1, 0] = keep.tile([P, M, J], BF16, name="grouped_w10", tag="grouped_w0", align_bytes=64)
-        nc.gpsimd.tensor_scalar(grouped_w[1, 0][:], raw_w[1, 0][:].rearrange("p j n -> p n j"), 1.0, 0.0, MULT, ADD)
-        round_w(1, 1, nc.vector.tensor_copy)
+        grouped_w[1] = keep.tile([P, N, J], BF16, name="grouped_w1", tag="grouped_w", align_bytes=64)
+        nc.gpsimd.tensor_scalar(
+            grouped_w[1][:, halves[0], :], raw_w1[0][:].rearrange("p j n -> p n j"), 1.0, 0.0, MULT, ADD
+        )
+        round_w(nc.vector.tensor_copy, grouped_w[1][:, halves[1], :], raw_w1[1][:])
         codes = keep.tile([P, S], U32, name="codes", tag="raw_w10", align_bytes=64)
         quantize_w(1, 0)
         quantize(1, hi)
@@ -140,8 +140,9 @@ def tile_picked_pair_lin_gate_sub_e_kernel(tc, xT, w, b, offs, out):
         quantize(1, lo)
         product(1, 0, lo, 4)
         product(1, 1, lo, 5)
-        round_w(0, 0, nc.vector.tensor_copy)
-        round_w(0, 1, nc.scalar.copy)
+        grouped_w[0] = keep.tile([P, N, J], BF16, name="grouped_w0", tag="grouped_w", align_bytes=64)
+        round_w(nc.vector.tensor_copy, grouped_w[0][:, 0:W0_ON_VECTOR, :], raw_w0[:, :, 0:W0_ON_VECTOR])
+        round_w(nc.scalar.copy, grouped_w[0][:, W0_ON_VECTOR:N, :], raw_w0[:, :, W0_ON_VECTOR:N])
         order = ((0, hi), (0, mid), (1, hi), (1, mid), (0, lo), (1, lo))
         for m, a in order:
             sigmoid(m, a)

@@ -21,7 +21,7 @@ J = 4
 M = 128
 PIECE = 256
 THIRD = S // 3
-LOAD_ORDER = (2, 0, 1, 3)
+WOVEN = 576
 W0_ON_VECTOR = 192
 
 
@@ -36,21 +36,23 @@ def tile_picked_pair_lin_gate_sub_e_kernel(tc, xT, w, b, offs, out):
         psum = ctx.enter_context(tc.psum_pool(name="psum", bufs=1))
 
         list_sb = keep.tile([P, S // 16], U16, name="list_sb")
-        planes = [keep.tile([P, T], F32, name=f"plane{j}") for j in range(J)]
+        first_planes = keep.tile([P, 2, T], F32, name="first_planes")
+        planes = [first_planes[:, j, :] for j in range(2)]
+        planes += [keep.tile([P, T], F32, name=f"plane{j}")[:] for j in range(2, J)]
         raw_w1 = [keep.tile([P, J, M], F32, name=f"raw_w1{m}", tag=f"raw_w1{m}", align_bytes=64) for m in range(2)]
         raw_w0 = keep.tile([P, J, N], F32, name="raw_w0")
-        bias = keep.tile([P, 2, 1], F32, name="bias")
+        bias = [keep.tile([P, 1], F32, name=f"bias{m}") for m in range(2)]
 
-        for j in LOAD_ORDER:
-            nc.sync.dma_start(planes[j][:], x_rows[:, j, :])
-            if j == LOAD_ORDER[0]:
-                nc.sync.dma_start(list_sb[:], offs)
+        nc.sync.dma_start(first_planes[:], x_rows[:, 0:2, :])
+        nc.sync.dma_start(list_sb[:], offs)
+        for j in range(2, J):
+            nc.sync.dma_start(planes[j], x_rows[:, j, :])
         for m in range(2):
             nc.sync.dma_start(raw_w1[m][:], w_rows[1][:, :, halves[m]])
         for rows in (slice(0, 2), slice(2, J)):
             nc.sync.dma_start(raw_w0[:, rows, :], w_rows[0][:, rows, :])
-        with nc.allow_non_contiguous_dma(reason="one bias value a partition for each half of the channels"):
-            nc.sync.dma_start(bias[:], b.rearrange("(m p) o -> p m o", p=P))
+        for m in range(2):
+            nc.sync.dma_start(bias[m][:], b[halves[m], :])
 
         warm = keep.tile([P, 1], F32, name="warm")
         warm_out = keep.tile([P, 1], F32, name="warm_out")
@@ -61,12 +63,18 @@ def tile_picked_pair_lin_gate_sub_e_kernel(tc, xT, w, b, offs, out):
         by_entry = grouped[:].rearrange("p (n j) -> p n j", j=J)
 
         def picked(j, a, z):
-            return planes[j][:].indirect(list_sb[:, a // 16 : z // 16])
+            return planes[j].indirect(list_sb[:, a // 16 : z // 16])
 
-        for j in LOAD_ORDER[:-1]:
-            cut = 2 * THIRD if j == 2 else V
-            nc.vector.tensor_copy(by_entry[:, cut:S, j], picked(j, cut, S))
-            nc.scalar.activation(by_entry[:, 0:cut, j], picked(j, 0, cut), COPY)
+        for j in range(2):
+            nc.vector.tensor_copy(by_entry[:, WOVEN:S, j], picked(j, WOVEN, S))
+        for a, z in ((0, WOVEN // 2), (WOVEN // 2, WOVEN)):
+            pairs = keep.tile([P, 2, z - a], F32, name=f"pairs{a}")
+            for j in range(2):
+                nc.scalar.activation(pairs[:, j, :], picked(j, a, z), COPY)
+            nc.gpsimd.tensor_scalar(by_entry[:, a:z, 0:2], pairs[:].rearrange("p j n -> p n j"), 1.0, 0.0, MULT, ADD)
+        j = 2
+        nc.vector.tensor_copy(by_entry[:, 2 * THIRD : S, j], picked(j, 2 * THIRD, S))
+        nc.scalar.activation(by_entry[:, 0 : 2 * THIRD, j], picked(j, 0, 2 * THIRD), COPY)
         j = J - 1
         nc.vector.tensor_copy(by_entry[:, 2 * THIRD : S, j], picked(j, 2 * THIRD, S))
         for a, z in ((THIRD, 2 * THIRD), (0, THIRD)):
@@ -120,7 +128,7 @@ def tile_picked_pair_lin_gate_sub_e_kernel(tc, xT, w, b, offs, out):
             )
 
         def sigmoid(m, a):
-            nc.scalar.activation(gate[m][:, a : a + PIECE], y[1, m, a], SIGMOID, bias=bias[:, m, :])
+            nc.scalar.activation(gate[m][:, a : a + PIECE], y[1, m, a], SIGMOID, bias=bias[m][:])
 
         hi, mid, lo = 2 * PIECE, PIECE, 0
         grouped_w[1] = keep.tile([P, N, J], BF16, name="grouped_w1", tag="grouped_w", align_bytes=64)

@@ -22,7 +22,7 @@ M = 128
 PIECE = 256
 THIRD = S // 3
 WOVEN = 576
-W0_ON_VECTOR = 192
+W0_ON_VECTOR = 160
 
 
 def tile_picked_pair_lin_gate_sub_e_kernel(tc, xT, w, b, offs, out):

@@ -141,17 +141,17 @@ def tile_picked_pair_lin_gate_sub_e_kernel(tc, xT, w, b, offs, out):
         quantize(1, hi)
         quantize_w(1, 1)
         product(1, 0, hi, 0)
-        product(1, 1, hi, 2)
+        product(1, 1, hi, 3)
         quantize(1, mid)
         product(1, 0, mid, 1)
-        product(1, 1, mid, 3)
+        product(1, 1, mid, 4)
         quantize(1, lo)
-        product(1, 0, lo, 4)
+        product(1, 0, lo, 2)
         product(1, 1, lo, 5)
         grouped_w[0] = keep.tile([P, N, J], BF16, name="grouped_w0", tag="grouped_w", align_bytes=64)
         round_w(nc.vector.tensor_copy, grouped_w[0][:, 0:W0_ON_VECTOR, :], raw_w0[:, :, 0:W0_ON_VECTOR])
         round_w(nc.scalar.copy, grouped_w[0][:, W0_ON_VECTOR:N, :], raw_w0[:, :, W0_ON_VECTOR:N])
-        order = ((0, hi), (0, mid), (1, hi), (1, mid), (0, lo), (1, lo))
+        order = [(m, a) for m in range(2) for a in (hi, mid, lo)]
         for m, a in order:
             sigmoid(m, a)
         quantize(0, hi)
@@ -159,11 +159,11 @@ def tile_picked_pair_lin_gate_sub_e_kernel(tc, xT, w, b, offs, out):
         product(0, 0, hi, 6)
         quantize(0, mid)
         product(0, 0, mid, 7)
-        quantize_w(0, 1)
-        product(0, 1, hi, 0)
-        product(0, 1, mid, 1)
         quantize(0, lo)
-        product(0, 0, lo, 2)
+        product(0, 0, lo, 0)
+        quantize_w(0, 1)
+        product(0, 1, hi, 1)
+        product(0, 1, mid, 2)
         product(0, 1, lo, 3)
 
         for m, a in order:

@@ -40,7 +40,8 @@ def tile_picked_pair_lin_gate_sub_e_kernel(tc, xT, w, b, offs, out):
         planes = [first_planes[:, j, :] for j in range(2)]
         planes += [keep.tile([P, T], F32, name=f"plane{j}")[:] for j in range(2, J)]
         raw_w1 = [keep.tile([P, J, M], F32, name=f"raw_w1{m}", tag=f"raw_w1{m}", align_bytes=64) for m in range(2)]
-        raw_w0 = keep.tile([P, J, N], F32, name="raw_w0")
+        w0_cuts = (slice(0, W0_ON_VECTOR), slice(W0_ON_VECTOR, N))
+        raw_w0 = [keep.tile([P, J, c.stop - c.start], F32, name=f"raw_w0{i}") for i, c in enumerate(w0_cuts)]
         bias = [keep.tile([P, 1], F32, name=f"bias{m}") for m in range(2)]
 
         nc.sync.dma_start(first_planes[:], x_rows[:, 0:2, :])
@@ -49,8 +50,8 @@ def tile_picked_pair_lin_gate_sub_e_kernel(tc, xT, w, b, offs, out):
             nc.sync.dma_start(planes[j], x_rows[:, j, :])
         for m in range(2):
             nc.sync.dma_start(raw_w1[m][:], w_rows[1][:, :, halves[m]])
-        for rows in (slice(0, 2), slice(2, J)):
-            nc.sync.dma_start(raw_w0[:, rows, :], w_rows[0][:, rows, :])
+        for raw, cols in zip(raw_w0, w0_cuts):
+            nc.sync.dma_start(raw[:], w_rows[0][:, :, cols])
         for m in range(2):
             nc.sync.dma_start(bias[m][:], b[halves[m], :])
 
@@ -67,17 +68,16 @@ def tile_picked_pair_lin_gate_sub_e_kernel(tc, xT, w, b, offs, out):
 
         for j in range(2):
             nc.vector.tensor_copy(by_entry[:, WOVEN:S, j], picked(j, WOVEN, S))
-        for a, z in ((0, WOVEN // 2), (WOVEN // 2, WOVEN)):
-            pairs = keep.tile([P, 2, z - a], F32, name=f"pairs{a}")
-            for j in range(2):
-                nc.scalar.activation(pairs[:, j, :], picked(j, a, z), COPY)
-            nc.gpsimd.tensor_scalar(by_entry[:, a:z, 0:2], pairs[:].rearrange("p j n -> p n j"), 1.0, 0.0, MULT, ADD)
+        pairs = keep.tile([P, 2, WOVEN], F32, name="pairs")
+        for j in range(2):
+            nc.scalar.activation(pairs[:, j, :], picked(j, 0, WOVEN), COPY)
+        nc.gpsimd.tensor_scalar(by_entry[:, 0:WOVEN, 0:2], pairs[:].rearrange("p j n -> p n j"), 1.0, 0.0, MULT, ADD)
         j = 2
         nc.vector.tensor_copy(by_entry[:, 2 * THIRD : S, j], picked(j, 2 * THIRD, S))
         nc.scalar.activation(by_entry[:, 0 : 2 * THIRD, j], picked(j, 0, 2 * THIRD), COPY)
         j = J - 1
         nc.vector.tensor_copy(by_entry[:, 2 * THIRD : S, j], picked(j, 2 * THIRD, S))
-        for a, z in ((THIRD, 2 * THIRD), (0, THIRD)):
+        for a, z in ((PIECE, 2 * THIRD), (0, PIECE)):
             nc.scalar.activation(by_entry[:, a:z, j], picked(j, a, z), COPY)
 
         w_codes = [keep.tile([P, N], U32, name=f"w_codes{d}", align_bytes=64) for d in range(2)]
@@ -141,29 +141,30 @@ def tile_picked_pair_lin_gate_sub_e_kernel(tc, xT, w, b, offs, out):
         quantize(1, hi)
         quantize_w(1, 1)
         product(1, 0, hi, 0)
-        product(1, 1, hi, 3)
+        product(1, 1, hi, 2)
         quantize(1, mid)
         product(1, 0, mid, 1)
-        product(1, 1, mid, 4)
-        quantize(1, lo)
-        product(1, 0, lo, 2)
-        product(1, 1, lo, 5)
+        product(1, 1, mid, 3)
         grouped_w[0] = keep.tile([P, N, J], BF16, name="grouped_w0", tag="grouped_w", align_bytes=64)
-        round_w(nc.vector.tensor_copy, grouped_w[0][:, 0:W0_ON_VECTOR, :], raw_w0[:, :, 0:W0_ON_VECTOR])
-        round_w(nc.scalar.copy, grouped_w[0][:, W0_ON_VECTOR:N, :], raw_w0[:, :, W0_ON_VECTOR:N])
-        order = [(m, a) for m in range(2) for a in (hi, mid, lo)]
-        for m, a in order:
-            sigmoid(m, a)
+        for copy, raw, cols in zip((nc.vector.tensor_copy, nc.scalar.copy), raw_w0, w0_cuts):
+            round_w(copy, grouped_w[0][:, cols, :], raw[:])
         quantize(0, hi)
         quantize_w(0, 0)
-        product(0, 0, hi, 6)
+        product(0, 0, hi, 4)
         quantize(0, mid)
-        product(0, 0, mid, 7)
-        quantize(0, lo)
-        product(0, 0, lo, 0)
+        product(0, 0, mid, 5)
+        quantize(1, lo)
+        product(1, 0, lo, 6)
+        order = ((0, hi), (0, mid), (1, hi), (1, mid), (0, lo), (1, lo))
+        for m, a in order[:5]:
+            sigmoid(m, a)
         quantize_w(0, 1)
-        product(0, 1, hi, 1)
-        product(0, 1, mid, 2)
+        product(0, 1, hi, 7)
+        product(0, 1, mid, 0)
+        product(1, 1, lo, 1)
+        sigmoid(1, lo)
+        quantize(0, lo)
+        product(0, 0, lo, 2)
         product(0, 1, lo, 3)
 
         for m, a in order:

from contextlib import ExitStack

import concourse.mybir as mybir

K, T, S, V, N = 512, 4096, 1536, 768, 256
FLOPS = 2 * K * N * S

F32 = mybir.dt.float32
BF16 = mybir.dt.bfloat16
U16 = mybir.dt.uint16
U32 = mybir.dt.uint32
U8 = mybir.dt.uint8
FP8X4 = mybir.dt.float8_e4m3fn_x4
MULT = mybir.AluOpType.mult
ADD = mybir.AluOpType.add
SIGMOID = mybir.ActivationFunctionType.Sigmoid
COPY = mybir.ActivationFunctionType.Copy

P = 128
J = 4
M = 128
PIECE = 256
THIRD = S // 3
WOVEN = 576
W0_ON_VECTOR = 160


def tile_picked_pair_lin_gate_sub_e_kernel(tc, xT, w, b, offs, out):
    nc = tc.nc
    x_rows = xT.rearrange("(p j) t -> p j t", j=J)
    w_rows = [w[d].rearrange("(p j) n -> p j n", j=J) for d in range(2)]
    halves = (slice(0, M), slice(M, N))

    with ExitStack() as ctx:
        keep = ctx.enter_context(tc.tile_pool(name="keep", bufs=1))
        psum = ctx.enter_context(tc.psum_pool(name="psum", bufs=1))

        list_sb = keep.tile([P, S // 16], U16, name="list_sb")
        first_planes = keep.tile([P, 2, T], F32, name="first_planes")
        planes = [first_planes[:, j, :] for j in range(2)]
        planes += [keep.tile([P, T], F32, name=f"plane{j}")[:] for j in range(2, J)]
        raw_w1 = [keep.tile([P, J, M], F32, name=f"raw_w1{m}", tag=f"raw_w1{m}", align_bytes=64) for m in range(2)]
        w0_cuts = (slice(0, W0_ON_VECTOR), slice(W0_ON_VECTOR, N))
        raw_w0 = [keep.tile([P, J, c.stop - c.start], F32, name=f"raw_w0{i}") for i, c in enumerate(w0_cuts)]
        bias = [keep.tile([P, 1], F32, name=f"bias{m}") for m in range(2)]

        nc.sync.dma_start(first_planes[:], x_rows[:, 0:2, :])
        nc.sync.dma_start(list_sb[:], offs)
        for j in range(2, J):
            nc.sync.dma_start(planes[j], x_rows[:, j, :])
        for m in range(2):
            nc.sync.dma_start(raw_w1[m][:], w_rows[1][:, :, halves[m]])
        for raw, cols in zip(raw_w0, w0_cuts):
            nc.sync.dma_start(raw[:], w_rows[0][:, :, cols])
        for m in range(2):
            nc.sync.dma_start(bias[m][:], b[halves[m], :])

        warm = keep.tile([P, 1], F32, name="warm")
        warm_out = keep.tile([P, 1], F32, name="warm_out")
        nc.vector.memset(warm[:], 0.0)
        nc.scalar.activation(warm_out[:], warm[:], SIGMOID)

        grouped = keep.tile([P, S * J], BF16, name="grouped", align_bytes=64)
        by_entry = grouped[:].rearrange("p (n j) -> p n j", j=J)

        def picked(j, a, z):
            return planes[j].indirect(list_sb[:, a // 16 : z // 16])

        for j in range(2):
            nc.vector.tensor_copy(by_entry[:, WOVEN:S, j], picked(j, WOVEN, S))
        pairs = keep.tile([P, 2, WOVEN], F32, name="pairs")
        for j in range(2):
            nc.scalar.activation(pairs[:, j, :], picked(j, 0, WOVEN), COPY)
        nc.gpsimd.tensor_scalar(by_entry[:, 0:WOVEN, 0:2], pairs[:].rearrange("p j n -> p n j"), 1.0, 0.0, MULT, ADD)
        j = 2
        nc.vector.tensor_copy(by_entry[:, 2 * THIRD : S, j], picked(j, 2 * THIRD, S))
        nc.scalar.activation(by_entry[:, 0 : 2 * THIRD, j], picked(j, 0, 2 * THIRD), COPY)
        j = J - 1
        nc.vector.tensor_copy(by_entry[:, 2 * THIRD : S, j], picked(j, 2 * THIRD, S))
        for a, z in ((PIECE, 2 * THIRD), (0, PIECE)):
            nc.scalar.activation(by_entry[:, a:z, j], picked(j, a, z), COPY)

        w_codes = [keep.tile([P, N], U32, name=f"w_codes{d}", align_bytes=64) for d in range(2)]
        w_scales = [keep.tile([P, N], U8, name=f"w_scales{d}", align_bytes=64) for d in range(2)]
        grouped_w = {}

        def round_w(copy, grouped_cols, rows):
            copy(
                grouped_cols.rearrange("p (c i) j -> p c j i", i=4),
                rows.rearrange("p j (c i) -> p c j i", i=4),
            )

        def quantize_w(d, m):
            nc.vector.quantize_mx(
                out=w_codes[d][:, halves[m]].bitcast(FP8X4),
                scales=w_scales[d][:, halves[m]],
                in_=grouped_w[d][:, halves[m], :].rearrange("p n j -> p (n j)"),
            )

        scales = keep.tile([P, S], U8, name="scales", align_bytes=64)
        gate = [keep.tile([P, V], F32, name=f"gate{m}") for m in range(2)]
        result = keep.tile([P, 2, V], F32, name="result")
        out_rows = out.rearrange("(m p) v -> p m v", p=P)
        y = {}

        def words(a, z):
            return codes[:, a:z].bitcast(FP8X4)

        def quantize(d, a):
            first = d * V + a
            nc.vector.quantize_mx(
                out=words(first, first + PIECE),
                scales=scales[:, first : first + PIECE],
                in_=grouped[:, J * first : J * (first + PIECE)],
            )

        def product(d, m, a, bank):
            first = d * V + a
            y[d, m, a] = psum.tile([P, PIECE], F32, name=f"y{d}_{m}_{a}", tag=f"bank{bank}")[:]
            nc.tensor.matmul_mx(
                out=y[d, m, a],
                lhsT=w_codes[d][:, halves[m]].bitcast(FP8X4),
                lhsT_scale=w_scales[d][:, halves[m]],
                rhs=words(first, first + PIECE),
                rhs_scale=scales[:, first : first + PIECE],
                start=True,
                stop=True,
            )

        def sigmoid(m, a):
            nc.scalar.activation(gate[m][:, a : a + PIECE], y[1, m, a], SIGMOID, bias=bias[m][:])

        hi, mid, lo = 2 * PIECE, PIECE, 0
        grouped_w[1] = keep.tile([P, N, J], BF16, name="grouped_w1", tag="grouped_w", align_bytes=64)
        nc.gpsimd.tensor_scalar(
            grouped_w[1][:, halves[0], :], raw_w1[0][:].rearrange("p j n -> p n j"), 1.0, 0.0, MULT, ADD
        )
        round_w(nc.vector.tensor_copy, grouped_w[1][:, halves[1], :], raw_w1[1][:])
        codes = keep.tile([P, S], U32, name="codes", tag="raw_w10", align_bytes=64)
        quantize_w(1, 0)
        quantize(1, hi)
        quantize_w(1, 1)
        product(1, 0, hi, 0)
        product(1, 1, hi, 2)
        quantize(1, mid)
        product(1, 0, mid, 1)
        product(1, 1, mid, 3)
        grouped_w[0] = keep.tile([P, N, J], BF16, name="grouped_w0", tag="grouped_w", align_bytes=64)
        for copy, raw, cols in zip((nc.vector.tensor_copy, nc.scalar.copy), raw_w0, w0_cuts):
            round_w(copy, grouped_w[0][:, cols, :], raw[:])
        quantize(0, hi)
        quantize_w(0, 0)
        product(0, 0, hi, 4)
        quantize(0, mid)
        product(0, 0, mid, 5)
        quantize(1, lo)
        product(1, 0, lo, 6)
        order = ((0, hi), (0, mid), (1, hi), (1, mid), (0, lo), (1, lo))
        for m, a in order[:5]:
            sigmoid(m, a)
        quantize_w(0, 1)
        product(0, 1, hi, 7)
        product(0, 1, mid, 0)
        product(1, 1, lo, 1)
        sigmoid(1, lo)
        quantize(0, lo)
        product(0, 0, lo, 2)
        product(0, 1, lo, 3)

        for m, a in order:
            cols = slice(a, a + PIECE)
            nc.vector.tensor_tensor(result[:, m, cols], y[0, m, a], gate[m][:, cols], MULT)
            nc.sync.dma_start(out_rows[:, m, cols], result[:, m, cols])
